import numpy as np, ml_dtypes
CORES = [2,3,42,43,82,83,122,123]
N = 8
BF = ml_dtypes.bfloat16
C, T, S, DQ = 1024, 256, 3, 1
PL = N * C; FREE = 31
RANGES = (("mem", 0, 63), ("h", 0, 63), ("pnd", 0, PL - 1), ("due", 0, FREE), ("val", 0, 63), ("w", 0, 255), ("kap", 0, 255), ("th", 0, 1008))
def parts(rng):
    tops = rng.integers(24, 64, (1, 8, 16))
    nm = np.add.accumulate(rng.integers(1, PL // 16, (N, 8, T, 16)), axis=3) + rng.integers(0, PL, (N, 8, T, 1))
    nm = rng.permuted(nm & (PL - 1), axis=3)
    du = np.where(rng.random((N, 8, T, 16)) < 0.2, FREE, rng.integers(0, 9, (N, 8, T, 16))); du[..., :S] = FREE
    return {"mem": (rng.random((N, 8, 16, C)) * (tops[..., None] + 1)).astype(np.int64), "h": rng.integers(0, 64, (N, 8, 16, T)),
            "val": (rng.random((N, 8, 16, T, 16)) * (tops[..., None, None] + 1)).astype(np.int64), "nm": nm, "du": du,
            "w": rng.integers(0, 256, (N, 8, 16)), "kap": rng.integers(0, 256, (N, 8, 16)),
            "th": (np.sum(tops, axis=2) * (0.8 + 0.13 * rng.random((N, 8)))).astype(np.int64)}
def pack(p):
    bf = lambda a: np.ascontiguousarray(a).astype(np.float32).astype(BF)
    i4 = lambda a: np.ascontiguousarray(a).astype(np.int32)
    return {"mem": bf(p["mem"].reshape(N, 128, C)), "h": bf(p["h"].reshape(N, 128, T)),
            "pnd": i4(p["nm"].transpose(0, 1, 3, 2).reshape(N, 128, T)), "due": i4(p["du"].transpose(0, 1, 3, 2).reshape(N, 128, T)),
            "val": bf(p["val"].reshape(N, 128, 16 * T)), "w": i4(p["w"].reshape(N, 128, 1)), "kap": i4(p["kap"].reshape(N, 128, 1)),
            "th": i4(np.repeat(p["th"].reshape(N, 8, 1), 16, axis=2).reshape(N, 128, 1))}
def setup_inputs(rng):
    return pack(parts(rng))
def setup_inputs_corners(rng):
    p = parts(rng); s = np.arange(16); own = p["nm"]; mode = rng.integers(0, 7, (N, 8, T, 1)); mode[..., T - 1, 0] = 4; mode[..., 0, 0] = 1
    e = rng.integers(0, S + 1, (N, 8, T, 1)); q = rng.choice(np.array([0, 1, S - 1, S, 30]), (N, 8, T, 16))
    late = 30 - (rng.random((N, 8, T, 16)) * rng.integers(2, 16, (N, 8, T, 1))).astype(np.int64)
    border = C * rng.integers(0, N, (N, 8, T, 1)) - 8; border[..., T - 1, 0] = -8
    du = np.where(mode == 3, np.where(s == 15, 0, FREE), q); du = np.where(mode == 6, late, du)
    du = np.where(mode == 2, np.where(s == 15, e, 30), du); du = np.where(mode == 1, e, du); du = np.where(mode == 0, FREE, du)
    du[..., :S] = FREE
    nm = np.where(mode == 4, (border + s) & (PL - 1), own)
    nm = np.where(mode == 0, (PL - 1) * rng.integers(0, 2, (N, 8, T, 16)), nm)
    p["w"][:, 2] = 0; p["w"][:, 5] = 255; p["kap"][:, 3] = 0; p["kap"][:, 4] = 255; p["th"][:, 1] = 0; p["th"][:, 6] = 1008
    p["th"][1:3] = 1008
    z = slice(T - 8, T); nm[2, 2, z] = own[2, 2, z]; du[2, 2, z] = FREE; du[2, 2, z, 13] = 30; du[2, 2, z, 15] = 0
    p["val"][2, 2, :, z, 13] = 63; p["val"][2, 2, :, z, 15] = 0
    nm[1, 5] = own[1, 5]; du[1, 5, :, S:] = 30
    p["th"][0, 0] = 0; du[0, 0] = FREE
    for r in (0, N - 1):
        p["th"][r, 4] = 0; nm[r, 4] = own[0, 4]; du[r, 4] = FREE; du[r, 4, :, 15] = 0
    du[0, 4, :, 14] = 1
    p["nm"] = nm; p["du"] = du
    return pack(p)
def setup_inputs_crowd(rng):
    p = parts(rng); s = np.arange(16); i = np.arange(T).reshape(1, 1, T, 1); r = np.arange(N).reshape(N, 1, 1, 1)
    owner = rng.integers(0, N, (N, 8, 1, 1)); owner[:, 2] = 0; owner[:, 5] = N - 1; owner[N - 1] = 0
    col = np.broadcast_to(64 + i + 17 * s, (N, 8, T, 16)).copy(); far = (T * (r + 1) + i + 17 * s) % C
    col[:, 2] = far[:, 0]; col[:, 5] = far[:, 0]
    p["nm"] = C * owner + col
    du = np.zeros((N, 8, T, 16), np.int64); du[..., :S] = FREE; du[:, 2, :, 1::2] = FREE; du[N - 1, :, :, 1::2] = FREE; p["du"] = du
    p["w"][:, 2] = 0; p["w"][N - 1] = 0; p["th"][:] = 0
    return pack(p)
def edge(rng, a, b):
    k = rng.integers(0, 3, a)
    return 63 * np.where(k == 2, rng.integers(0, 2, b), k)
def setup_inputs_ends(rng):
    p = parts(rng); s = np.arange(16)
    mem = edge(rng, (N, 8, 1, C), (N, 8, 16, C)); mem[..., 0] = 0; mem[..., C - 1] = 63
    h = edge(rng, (N, 8, 1, T), (N, 8, 16, T)); val = edge(rng, (N, 8, 1, T, 16), (N, 8, 16, T, 16))
    for g in (1, 5, 7): mem[:, g, 3] = 0
    for g in (1, 5): val[:, g, 3] = 0
    w = 255 * rng.integers(0, 2, (N, 8, 16)); w[:, 1::2, 15] = 65; w[:, 6] = 255
    kap = 255 * rng.integers(0, 2, (N, 8, 16)); kap[:, 1::2, 15] = 255; kap[:, 1::2, 0] = 0
    th = 1008 * rng.integers(0, 2, (N, 8)); th[:, 0] = 0; th[:, 4] = 1008; th[:, 1::2] = 1008; th[0::2, 6] = 1008
    h[:, 1::2, :, T - 1] = 0; h[:, 1::2, 15, T - 1] = 63
    h[:, 6, :, T - 1] = 63; h[:, 0::4, :, T - 1] = 0
    few = rng.random((N, 8, T, 1)) < 0.7
    s1 = rng.integers(S, 16, (N, 8, T, 1)); s2 = S + (s1 - S + rng.integers(1, 16 - S, (N, 8, T, 1))) % (16 - S)
    nm = np.where(s == s1, 0, np.where(s == s2, PL - 1, (PL - 1) * rng.integers(0, 2, (N, 8, T, 16))))
    du = np.where(((s == s1) | (s == s2)) & (rng.random((N, 8, T, 16)) < 0.75), 0, FREE)
    nm = np.where(few, nm, p["nm"]); du = np.where(few, du, np.where((s >= S) & (rng.random((N, 8, T, 16)) < 0.6), 0, FREE))
    nm[:, 0::4, T - 1] = 0; du[:, 0::4, T - 1] = FREE
    u = (16 * 255 * 63) & 4095; e0 = ((u * u) >> 4) & (PL - 1); e1 = (((u * u) >> 4) + 255 * u) & (PL - 1)
    mem[e0 // C, 6, :, e0 % C] = 63; mem[e1 // C, 6, :, e1 % C] = 63
    nm[:, 6, T - 1] = e0; du[:, 6, T - 1] = FREE
    return pack({"mem": mem, "h": h, "val": val, "nm": nm, "du": du, "w": w, "kap": kap, "th": th})
def setup_inputs_meet(rng):
    p = parts(rng); b = np.array([0, 3, 4, 7]); e = np.array([1, 2, 5, 6]); gi = np.arange(8)[None, :, None]; s = np.arange(16)
    pool = p["nm"][0, :, 0].copy()
    nm = rng.permuted(np.broadcast_to(pool[None, :, None, :], (N, 8, T, 16)).copy(), axis=3); nm[:, 4] = pool[4]
    p["nm"][:, b] = nm[:, b]
    du = rng.integers(0, 3, (N, 8, T, 16)); dt = np.where(rng.random((N, 8, T, 16)) < 0.3, FREE, rng.integers(0, 2, (N, 8, T, 16)))
    du[:, e] = dt[:, e]; du[:, 4] = np.where((rng.random((N, T, 1)) < 0.2) & (s > S), FREE, 0); du[..., :S] = FREE; p["du"] = du
    pat = rng.integers(0, 4, (8, 6, 16)) * rng.choice(np.array([1, 3, 20]), (8, 1, 1))
    mem = pat[gi, rng.integers(0, 6, (N, 8, C))].transpose(0, 1, 3, 2)
    h = pat[gi, rng.integers(0, 6, (N, 8, T))].transpose(0, 1, 3, 2)
    val = pat[gi[..., None], rng.integers(0, 6, (N, 8, T, 16))].transpose(0, 1, 4, 2, 3)
    p["mem"][:, e] = mem[:, e]; p["h"][:, e] = h[:, e]; p["val"][:, e] = val[:, e]
    full = np.sum(np.max(pat, axis=1) - np.min(pat, axis=1), axis=1)
    off = rng.permuted(np.resize(np.array([0, 0, 1, -1, -3]), N * 4)).reshape(N, 4)
    p["th"][:, e] = np.maximum(full[e][None, :] + off, 0)
    p["th"][:, 0] = 0; p["th"][:, 4] = 0
    p["h"][:, 3] = p["h"][:1, 3, :, :1].copy(); p["w"][:, 3] = p["w"][:1, 3].copy(); p["kap"][:, 3] = p["kap"][:1, 3].copy()
    return pack(p)
def setup_inputs_spread(rng):
    p = parts(rng)
    p["mem"] = np.minimum((np.exp2(6 * rng.random((N, 8, 1, C))) * rng.random((N, 8, 16, C))).astype(np.int64), 63)
    p["h"] = np.minimum((np.exp2(6 * rng.random((N, 8, 1, T))) * rng.random((N, 8, 16, T))).astype(np.int64), 63)
    p["val"] = np.minimum((np.exp2(6 * rng.random((N, 8, 1, T, 16))) * rng.random((N, 8, 16, T, 16))).astype(np.int64), 63)
    p["w"] = np.minimum(np.exp2(8 * rng.random((N, 8, 16))).astype(np.int64), 255)
    p["th"] = rng.integers(0, 1009, (N, 8))
    du = np.where(rng.random((N, 8, T, 16)) < 0.5, rng.integers(0, 4, (N, 8, T, 16)), rng.integers(0, FREE + 1, (N, 8, T, 16))); du[..., :S] = FREE; p["du"] = du
    return pack(p)
def check_inputs(d):
    bad = []
    for k, lo, hi in RANGES:
        v = np.asarray(d[k]).astype(np.float64)
        if not (np.all(v >= lo) and np.all(v <= hi) and np.all(v == np.floor(v))): bad.append("range of " + k)
    du = np.asarray(d["due"]).astype(np.int64).reshape(N, 8, 16, T); nm = np.asarray(d["pnd"]).astype(np.int64).reshape(N, 8, 16, T)
    if np.any(du[:, :, :S] != FREE): bad.append("slots that start free")
    k = np.sort(np.where(du != FREE, nm, -1 - np.arange(16).reshape(1, 1, 16, 1)), axis=2)
    if np.any(k[:, :, 1:] == k[:, :, :-1]): bad.append("pending names of a thread differ")
    t = np.asarray(d["th"]).reshape(N, 8, 16)
    if np.any(t != t[:, :, :1]): bad.append("th alike in a group")
    return bad
def reference(mem, h, pnd, due, val, w, kap, th):
    whole = lambda a: a.astype(np.float32).astype(np.int64)
    mt = np.ascontiguousarray(whole(mem).reshape(N, 8, 16, C).transpose(1, 0, 3, 2)).reshape(8, PL, 16)
    hh = whole(h).reshape(N, 8, 16, T).transpose(0, 1, 3, 2)
    nm = pnd.astype(np.int64).reshape(N, 8, 16, T).transpose(0, 1, 3, 2).copy()
    du = due.astype(np.int64).reshape(N, 8, 16, T).transpose(0, 1, 3, 2).copy()
    vl = whole(val).reshape(N, 8, 16, T, 16).transpose(0, 1, 3, 4, 2).copy()
    ww = w.astype(np.int64).reshape(N, 8, 1, 16); kk = kap.astype(np.int64).reshape(N, 8, 1, 16); tt = th.astype(np.int64).reshape(N, 8, 16)[:, :, :1]
    A = np.zeros((N, 1, 1, 1), np.int64); s16 = np.arange(16); gi = np.arange(8).reshape(1, 8, 1, 1)
    for t in range(S):
        u = (np.sum(ww * hh, axis=3) & 4095)[..., None]
        z = ((u * u) >> 4) + kk * u + A
        a = np.where((s16 & 1) == 0, z, np.where(((z >> 3) & 1) == 1, nm + z, nm)) & (PL - 1)
        pend = du != FREE
        hit = (a[..., :, None] == nm[..., None, :]) & pend[..., None, :]
        x = np.where(np.any(hit, axis=4)[..., None], np.take_along_axis(vl, np.argmax(hit, axis=4)[..., None], 3), mt[gi, a])
        hi = np.max(x, axis=3); lo = np.min(x, axis=3); y = (hi + lo) >> 1
        score = np.sum(np.abs(x - hh[..., None, :]), axis=4)
        b = np.take_along_axis(a, np.argmax(score, axis=3)[..., None], 3)
        fence = np.sum(hi - lo, axis=3) >= tt
        same = (nm == b) & pend; had = np.any(same, axis=3)
        put = np.where(had[..., None], same, s16 == t) & ~fence[..., None]
        vl = np.where(put[..., None], y[..., None, :], vl); nm = np.where(put, b, nm)
        du[..., t] = np.where(~had & ~fence, t + 1 + (np.sum(y, axis=3) & DQ), du[..., t])
        sl = np.argmin(du, axis=3)[..., None]; least = np.take_along_axis(du, sl, 3)[..., 0]
        go = (least != FREE) & (fence | (least <= t))
        place = np.take_along_axis(nm, sl, 3)[..., 0]; value = np.take_along_axis(vl, sl[..., None], 3)[..., 0, :]
        du = np.where(go[..., None] & (s16 == sl), FREE, du)
        for g in range(8):
            m = go[:, g].reshape(-1); v = value[:, g].reshape(-1, 16)[m]
            first, at = np.unique(place[:, g].reshape(-1)[m], return_index=True)
            mt[g, first] = v[at]
        hh = np.abs(y - hh); A = (np.sum(fence, axis=(1, 2)) & 63).reshape(N, 1, 1, 1)
    bf = lambda e: np.ascontiguousarray(e).astype(np.float32).astype(BF)
    return {"ymem": bf(mt.reshape(8, N, C, 16).transpose(1, 0, 3, 2).reshape(N, 128, C)), "yh": bf(hh.transpose(0, 1, 3, 2).reshape(N, 128, T)),
            "ypnd": np.ascontiguousarray(nm.transpose(0, 1, 3, 2).reshape(N, 128, T)).astype(np.float32),
            "ydue": np.ascontiguousarray(du.transpose(0, 1, 3, 2).reshape(N, 128, T)).astype(np.float32),
            "yval": bf(vl.transpose(0, 1, 4, 2, 3).reshape(N, 128, 16 * T))}

@@ -1,0 +1,582 @@
+from concourse.bass import DstId, RemoteDMATransfer
+from concourse.mybir import dt, AluOpType as A, AxisListType, ActivationFunctionType as AF
+
+N, C, TH, S, STEPS = 8, 1024, 256, 16, 3
+PL = N * C
+VAL = PL
+DUM = PL + S * TH
+WC = DUM + TH
+HALF = 128
+
+SCRATCH = {
+    "win": ("sbuf", [128, WC], "bfloat16"),
+    "vali": ("sbuf", [128, 4096], "bfloat16"),
+    "hexp": ("sbuf", [128, 4096], "bfloat16"), "xs": ("sbuf", [128, 4096], "bfloat16"), "ab": ("sbuf", [128, 4096], "bfloat16"),
+    "hs": ("sbuf", [128, 4096], "bfloat16"), "lsc": ("sbuf", [128, 4096], "bfloat16"), "eqb": ("sbuf", [128, 4096], "bfloat16"),
+    "rstn": ("sbuf", [128, 2048], "bfloat16"), "rstp": ("sbuf", [128, 2048], "bfloat16"),
+    "idb": ("sbuf", [128, 128], "bfloat16"), "nidb": ("sbuf", [128, 128], "bfloat16"), "n2idb": ("sbuf", [128, 128], "bfloat16"),
+    "idf": ("sbuf", [128, 128], "float32"), "bob": ("sbuf", [128, 128], "bfloat16"),
+    "gib": ("sbuf", [128, 8], "bfloat16"), "ngib": ("sbuf", [128, 8], "bfloat16"), "gif": ("sbuf", [128, 8], "float32"),
+    "bs": ("sbuf", [128, 1024], "bfloat16"), "wh": ("sbuf", [128, 2048], "bfloat16"),
+    "onesb": ("sbuf", [128, 128], "bfloat16"), "onesf": ("sbuf", [128, 128], "float32"),
+    "cy": ("sbuf", [128, 256], "bfloat16"), "ckf": ("sbuf", [128, 128], "bfloat16"), "ck16": ("sbuf", [128, 128], "bfloat16"),
+    "we": ("sbuf", [128, 96], "bfloat16"), "lzo": ("sbuf", [128, 256], "float32"), "lze": ("sbuf", [128, 256], "float32"),
+    "thd": ("sbuf", [128, 16], "float32"), "iotp": ("sbuf", [128, 8], "int32"), "iotc": ("sbuf", [128, 256], "int32"),
+    "cg": ("sbuf", [128, 256], "int32"), "cm": ("sbuf", [128, 256], "int32"), "oc": ("sbuf", [128, 256], "float32"),
+    "colf": ("sbuf", [128, 16], "float32"), "coli": ("sbuf", [128, 16], "int32"),
+    "r01": ("sbuf", [128, 256], "float32"), "dm": ("sbuf", [128, 256], "float32"), "tri": ("sbuf", [128, 256], "float32"),
+    "w8": ("sbuf", [128, 24], "float32"), "tmp1": ("sbuf", [128, 256], "float32"), "tmp2": ("sbuf", [128, 256], "float32"),
+    "tmp3": ("sbuf", [128, 256], "float32"),
+    "wraw": ("sbuf", [128, 8], "int32"), "kraw": ("sbuf", [128, 8], "int32"), "traw": ("sbuf", [128, 8], "int32"),
+    "praw": ("sbuf", [128, 256], "int32"), "draw": ("sbuf", [128, 256], "int32"),
+    "hb0": ("sbuf", [128, 256], "bfloat16"), "hb1": ("sbuf", [128, 256], "bfloat16"),
+    "nmd": ("sbuf", [128, 256], "float32"), "nmo": ("sbuf", [128, 256], "float32"), "dk": ("sbuf", [128, 256], "float32"),
+    "hid": ("sbuf", [128, 256], "float32"), "r1": ("sbuf", [128, 256], "bfloat16"), "r2": ("sbuf", [128, 256], "bfloat16"),
+    "r1a": ("sbuf", [128, 256], "bfloat16"), "r2a": ("sbuf", [128, 256], "bfloat16"),
+    "ui": ("sbuf", [128, 128], "int32"), "um": ("sbuf", [128, 128], "int32"), "usq": ("sbuf", [128, 128], "int32"),
+    "rz": ("sbuf", [128, 128], "float32"), "zi": ("sbuf", [128, 256], "int32"), "bit": ("sbuf", [128, 256], "int32"),
+    "mz": ("sbuf", [128, 256], "float32"), "a0": ("sbuf", [128, 256], "int32"), "ai": ("sbuf", [128, 256], "int32"),
+    "off": ("sbuf", [128, 256], "float32"), "ou": ("sbuf", [128, 256], "uint16"),
+    "km": ("sbuf", [128, 256], "float32"), "zz": ("sbuf", [128, 256], "float32"), "oh": ("sbuf", [128, 256], "float32"),
+    "wb": ("sbuf", [128, 256], "float32"), "wm": ("sbuf", [128, 256], "float32"),
+    "pbu": ("sbuf", [128, 256], "uint16"), "pbm": ("sbuf", [128, 256], "float32"),
+    "km2": ("sbuf", [128, 256], "float32"), "rec": ("sbuf", [128, 256], "float32"), "ro": ("sbuf", [128, 256], "float32"),
+    "os": ("sbuf", [128, 256], "float32"), "zc": ("sbuf", [128, 256], "float32"), "dsc": ("sbuf", [128, 256], "float32"),
+    "sm": ("sbuf", [128, 640], "float32"), "si": ("sbuf", [128, 256], "int32"),
+    "l2": ("sbuf", [128, 16], "uint16"), "stl": ("sbuf", [128, 16], "uint16"),
+    "eb": ("sbuf", [128, 2304], "bfloat16"), "acol": ("sbuf", [128, 8], "float32"),
+    "yd": ("sbuf", [128, 256], "bfloat16"), "yb": ("sbuf", [128, 256], "bfloat16"),
+    "onm": ("sbuf", [128, 256], "float32"), "odu": ("sbuf", [128, 256], "float32"),
+}
+for _t in range(STEPS):
+    SCRATCH["lv%d" % _t] = ("sbuf", [128, N * TH], "bfloat16")
+    SCRATCH["ln%d" % _t] = ("sbuf", [128, N * 16], "uint16")
+PSUM = ["pa", "pb", "pc", "pv", "pz", "py", "pk", "ps"]
+for _n in PSUM:
+    SCRATCH[_n] = ("psum", [128, 512], "float32")
+NDMA = 16
+SEMAPHORES = ["sv", "ss", "sp", "sg", "ag", "la"] + ["d%d" % k for k in range(NDMA)]
+SEMAPHORES += [n + "_%d" % t for t in range(STEPS) for n in ("lv", "ln")]
+SEMAPHORES += ["x%d_%d" % (t, r) for t in range(STEPS) for r in range(N)]
+
+
+def rank_program(g, core, T, topo):
+    rank = T.rank_of(core)
+    if rank is None:
+        return
+    Q = {"v": g.vector, "s": g.scalar, "p": g.tensor, "g": g, "y": g.sync}
+    SEM = {"v": "sv", "s": "ss", "p": "sp", "g": "sg"}
+    cnt = {q: 0 for q in Q}
+    clock = {q: {} for q in Q}
+    snap = {}
+    hist = {}
+    ndma = [0]
+    held = {}
+
+    def B(name, c0=0, c1=None, step=1, p0=0, p1=128):
+        if c1 is None:
+            c1 = SCRATCH[name][1][1]
+        return (name, p0, p1, c0, c1, step)
+
+    def ap(b):
+        if b[5] == 1:
+            return T[b[0]][b[1]:b[2], b[3]:b[4]]
+        return T[b[0]][b[1]:b[2], b[3]:b[4]:b[5]]
+
+    def wait(q, sem, val):
+        if clock[q].get(sem, 0) >= val:
+            return
+        Q[q].wait_ge(T.sem[sem], val)
+        for k, v in snap.get((sem, val), {}).items():
+            if clock[q].get(k, 0) < v:
+                clock[q][k] = v
+        clock[q][sem] = val
+
+    def deps(q, outs, ins):
+        need = {}
+        for b, w in [(o, True) for o in outs] + [(i, False) for i in ins]:
+            bank = b[0] in PSUM
+            for (c0, c1, hw, hq, tok, st) in hist.get(b[0], []):
+                if not bank and (c1 <= b[3] or b[4] <= c0):
+                    continue
+                if not bank and st == b[5] and (c0 - b[3]) % st:
+                    continue
+                if not (w or hw) and not (bank and hq != q):
+                    continue
+                if hq == q and q != "y":
+                    if not hw or q == "p":
+                        continue
+                    if bank and (c1 <= b[3] or b[4] <= c0):
+                        continue
+                if need.get(tok[0], 0) < tok[1]:
+                    need[tok[0]] = tok[1]
+        for sem in sorted(need):
+            wait(q, sem, need[sem])
+
+    def note(q, outs, ins, tok):
+        snap[tok] = dict(clock[q])
+        held[tok[0]] = tok[1]
+        for b, w in [(o, True) for o in outs] + [(i, False) for i in ins]:
+            h = hist.setdefault(b[0], [])
+            keep = []
+            for e in h:
+                if w and b[5] == 1 and b[2] - b[1] == 128 and b[3] <= e[0] and e[1] <= b[4] and b[0] not in PSUM and not (e[3] == "y"):
+                    continue
+                if e[3] == q and q in SEM and e[2] == w and e[0] == b[3] and e[1] == b[4] and e[5] == b[5]:
+                    continue
+                keep.append(e)
+            keep.append((b[3], b[4], w, q, tok, b[5]))
+            hist[b[0]] = keep
+
+    def op(q, fn, outs, ins):
+        deps(q, outs, ins)
+        cnt[q] += 1
+        fn().then_inc(T.sem[SEM[q]], 1)
+        note(q, outs, ins, (SEM[q], cnt[q]))
+
+    def dma(q, out, in_, outs, ins):
+        deps(q, outs, ins)
+        sem = "d%d" % ndma[0]
+        ndma[0] += 1
+        Q[q].dma_start(out, in_).then_inc(T.sem[sem], 16)
+        note("y", outs, ins, (sem, 16))
+
+    def cp(o, i):
+        op("v", lambda: g.vector.tensor_copy(ap(o), ap(i)), [o], [i])
+
+    def tt(o, a, b, f):
+        op("v", lambda: g.vector.tensor_tensor(ap(o), ap(a), ap(b), f), [o], [a, b])
+
+    def ts(o, a, s1, f1, s2=None, f2=None):
+        x1 = ap(s1) if isinstance(s1, tuple) else s1
+        x2 = ap(s2) if isinstance(s2, tuple) else s2
+        ins = [a] + [s for s in (s1, s2) if isinstance(s, tuple)]
+        if f2 is None:
+            op("v", lambda: g.vector.tensor_scalar(ap(o), ap(a), x1, None, f1), [o], ins)
+        else:
+            op("v", lambda: g.vector.tensor_scalar(ap(o), ap(a), x1, x2, f1, f2), [o], ins)
+
+    def fill(o, c):
+        op("v", lambda: g.vector.memset(ap(o), c), [o], [])
+
+    def scan(o, d0, d1, f0, f1):
+        op("v", lambda: g.vector.tensor_tensor_scan(ap(o), ap(d0), ap(d1), 0.0, f0, f1), [o], [d0, d1])
+
+    def act(o, i, f, bias=0.0, scale=1.0):
+        op("s", lambda: g.scalar.activation(ap(o), ap(i), f, bias=bias, scale=scale), [o], [i])
+
+    def mm(o, l, r, st, sp):
+        op("p", lambda: g.tensor.matmul(ap(o), ap(l), ap(r), st, sp), [o], [l, r])
+
+    def iota(o, pat, base, cm):
+        op("g", lambda: g.iota(ap(o), pat, base, cm), [o], [])
+
+    def sm(k):
+        return B("sm", 16 * k, 16 * k + 16)
+
+    def si(k):
+        return B("si", 16 * k, 16 * k + 16)
+
+    def ends(n):
+        return B(n, 15, 256, 16)
+
+    def starts(n):
+        return B(n, 0, 256, 16)
+
+    win = B("win")
+    own = B("win", rank * C, rank * C + C)
+
+    def send(b, sem, loc):
+        others = [c for c in T.cores if c != core]
+        far = [c for c in others if topo.chip(c) != topo.chip(core)]
+        near = [c for c in others if topo.chip(c) == topo.chip(core)]
+        ef = topo.engines(core, far[0])
+        en = [e for e in topo.engines(core, near[0]) if e not in ef]
+        deps("g", [], [b])
+        trs = []
+        for dst, eng in ((far, ef), (near, en)):
+            ids = []
+            for c in dst:
+                rid, pid, _ = topo.addr(c)
+                ids.append(DstId(rid=rid, pnc=pid))
+            trs.append(RemoteDMATransfer(dst_ids=ids, dma_engine_mask=sum(1 << e for e in eng), remote_sem=T.sem[sem],
+                                         srcs=[ap(b)], dsts=[ap(b)] * len(ids), alu_op=0))
+        g.remote_dma_fused(trs, local_sem=T.sem[loc])
+        note("y", [], [b], (loc, len(ef) + len(en)))
+
+    def arrives(src):
+        ef = topo.engines(src, [c for c in T.cores if topo.chip(c) != topo.chip(src)][0])
+        if topo.chip(src) != topo.chip(core):
+            return len(ef)
+        return len([e for e in topo.engines(src, core) if e not in ef])
+
+    dma("y", ap(own), T.mem[:], [own], [])
+    dma("s", T.hb0[:], T.h[:], [B("hb0")], [])
+    dma("y", T.praw[:], T.pnd[:], [B("praw")], [])
+    dma("s", T.draw[:], T.due[:], [B("draw")], [])
+    dma("y", T.wraw[:, 0:1], T.w[:], [B("wraw")], [])
+    dma("s", T.kraw[:, 0:1], T.kap[:], [B("kraw")], [])
+    dma("y", T.traw[:, 0:1], T.th[:], [B("traw")], [])
+    dma("s", T.vali[:], T.val[:], [B("vali")], [])
+    iota(B("iotp", 0, 1), [[0, 1]], 0, 1)
+    iota(B("iotc"), [[1, 256]], 0, 0)
+    send(own, "ag", "la")
+
+    PF, PG, PM, PS, WCOL, KCOL, TCOL = [B("colf", k, k + 1) for k in range(7)]
+    cp(PF, B("iotp", 0, 1))
+    ts(B("coli", 0, 1), B("iotp", 0, 1), 4, A.arith_shift_right)
+    ts(B("coli", 1, 2), B("iotp", 0, 1), 15, A.bitwise_and)
+    ts(B("cg"), B("iotc"), 4, A.arith_shift_right)
+    ts(B("cm"), B("iotc"), 15, A.bitwise_and)
+    cp(PG, B("coli", 0, 1))
+    cp(PM, B("coli", 1, 2))
+    ts(PS, PM, 1.0 / 512, A.mult)
+    ts(B("idf"), B("iotc", 0, 128), PF, A.is_equal)
+    ts(B("idb"), B("iotc", 0, 128), PF, A.is_equal)
+    ts(B("bob"), B("cg", 0, 128), PG, A.is_equal)
+    ts(B("gib"), B("iotc", 0, 8), PG, A.is_equal)
+    ts(B("gif"), B("iotc", 0, 8), PG, A.is_equal)
+    ts(B("r01"), B("cm"), 0, A.not_equal)
+    ts(B("dm"), B("cm"), PM, A.is_equal)
+    cp(B("tmp1"), B("praw"))
+    ts(B("tmp2"), B("draw"), 1.0 / 32, A.mult, PS, A.add)
+    for q in range(2):
+        mm(B("ps", 128 * q, 128 * q + 128), B("tmp1", 128 * q, 128 * q + 128), B("idf"), True, True)
+        mm(B("ps", 256 + 128 * q, 384 + 128 * q), B("tmp2", 128 * q, 128 * q + 128), B("idf"), True, True)
+    act(B("nmd"), B("ps", 0, 256), AF.Copy)
+    act(B("dk"), B("ps", 256, 512), AF.Copy)
+    ts(B("onesb"), B("idb"), 0.0, A.mult, 1.0, A.add)
+    fill(B("onesf"), 1.0)
+    cp(WCOL, B("wraw", 0, 1))
+    cp(KCOL, B("kraw", 0, 1))
+    cp(TCOL, B("traw", 0, 1))
+    fill(B("we"), 0.0)
+    for q in range(2):
+        for z in (0, 32):
+            ts(B("we", 48 * q + z + 8 * q, 48 * q + z + 8 * q + 8), B("gib"), WCOL, A.mult)
+    ts(B("zi"), B("cm"), 1, A.bitwise_and)
+    cp(B("oc"), B("zi"))
+    ts(B("tmp3", 0, 128), B("idf"), KCOL, A.mult)
+    ts(B("tmp3", 128, 136), B("gif"), TCOL, A.mult, 1.0 / 16, A.mult)
+    mm(B("pk", 0, 128), B("onesf"), B("tmp3", 0, 128), True, True)
+    mm(B("pk", 128, 136), B("onesf"), B("tmp3", 128, 136), True, True)
+    for q in range(2):
+        o = B("mz", 128 * q, 128 * q + 128, 1, 0, 48)
+        x = B("off", 128 * q, 128 * q + 128, 1, 0, 48)
+        cgs = B("cg", 0, 128, 1, 0, 48)
+        pfs = B("colf", 0, 1, 1, 0, 48)
+        ts(o, cgs, 8.0 * q, A.add, pfs, A.is_equal)
+        tt(o, B("pk", 0, 128, 1, 0, 48), o, A.mult)
+        ts(x, cgs, 8.0 * q + 32, A.add, pfs, A.is_equal)
+        tt(o, o, x, A.add)
+        zo, ze = [B(n, 128 * q, 128 * q + 128, 1, 0, 48) for n in ("lzo", "lze")]
+        tt(zo, o, B("oc", 0, 128, 1, 0, 48), A.mult)
+        tt(ze, o, zo, A.subtract)
+        cp(B("thd", 8 * q, 8 * q + 8), B("pk", 128, 136))
+    fill(B("rz"), 0.0)
+    fill(B("acol"), 0.0)
+    cp(B("zi"), B("nmd"))
+    ts(B("a0"), B("zi"), 7, A.arith_shift_right)
+    ts(B("bit"), B("zi"), 127, A.bitwise_and)
+    cp(B("hid"), B("a0"))
+    cp(B("r1", 1, 256, 2), B("bit", 0, 256, 2))
+    cp(B("r2", 1, 256, 2), B("bit", 1, 256, 2))
+    tt(B("nmo"), B("nmd"), B("oc"), A.mult)
+    ts(B("w8", 0, 8), B("iotc", 0, 16, 2), PM, A.is_equal, 128.0, A.mult)
+    ts(B("w8", 8, 16), B("iotc", 1, 16, 2), PM, A.is_equal)
+    tt(B("w8", 16, 24), B("w8", 0, 8), B("w8", 8, 16), A.add)
+    for q in range(8):
+        ts(B("bs", 128 * q, 128 * q + 128), B("bob"), B("w8", 16 + q, 17 + q), A.mult)
+    for s in range(S):
+        ts(B("wh", 128 * s, 128 * s + 128), B("idb"), 256.0 * (64 + s), A.mult)
+    fill(B("cy", 0, 256, 1, 0, 2), -8192.0)
+    cp(B("cy", 0, 256, 1, 0, 1), B("iotc", 0, 256, 1, 0, 1))
+    ts(B("ckf", 0, 128, 1, 0, 1), B("cm", 0, 128, 1, 0, 1), -1.0 / 16, A.mult, 15.0 / 16, A.add)
+    ts(B("ck16", 0, 128, 1, 0, 1), B("cm", 0, 128, 1, 0, 1), 16384.0, A.mult)
+    ts(B("tri"), B("cm"), PM, A.is_gt)
+    ts(B("nidb"), B("idb"), -1.0, A.mult)
+    ts(B("n2idb"), B("idb"), -2.0, A.mult)
+    ts(B("ngib"), B("gib"), -1.0, A.mult)
+    ts(sm(0), B("iotc", 0, 16), 16.0, A.mult, PM, A.add)
+    ts(sm(1), sm(0), 1.0 * DUM, A.add)
+    for t in range(STEPS):
+        ts(sm(2 + t), sm(0), 1.0 * VAL + TH * t, A.add)
+    ts(sm(5), sm(0), 1.0 * VAL, A.add)
+    fill(B("rstp"), 0.0)
+    fill(B("rstn"), 0.0)
+    fill(B("rstp", 0, 2048, 16), 256.0)
+    fill(B("rstn", 0, 2048, 16), -256.0)
+    fill(B("zz"), 0.0)
+    fill(B("zc"), 0.0)
+
+    def spread_h(h):
+        for k in range(S):
+            act(B("hexp", k, 4096, 16), h, AF.Copy)
+
+    spread_h(B("hb0"))
+    for s in range(S):
+        act(B("win", VAL + TH * s, VAL + TH * s + TH), B("vali", s, 4096, 16), AF.Copy)
+
+    def bcast(dst):
+        scan(dst, B("r01"), B("zz"), A.mult, A.add)
+
+    def to_lists(dst, src_m):
+        for q in range(2):
+            mm(B(dst[0], dst[3] + 8 * q, dst[3] + 8 * q + 8), B(src_m, 128 * q, 128 * q + 128), B("gif"), True, True)
+
+    def scatter_all(t):
+        for r in range(N - 1, -1, -1):
+            lv, ln = B("lv%d" % t, TH * r, TH * r + TH), B("ln%d" % t, 16 * r, 16 * r + 16)
+            if r != rank:
+                wait("v", "x%d_%d" % (t, r), 2 * arrives(T.cores[r]))
+            op("v", lambda: g.vector.tensor_copy(ap(win).indirect(ap(ln)), ap(lv)), [win], [lv, ln])
+
+    def early_drain(t):
+        scan(B("km"), B("rstp", 0, 256), B("dk"), A.add, A.min)
+        cp(starts("zz"), ends("km"))
+        bcast(B("pv", 0, 256))
+        tt(B("oh"), B("pv", 0, 256), B("dk"), A.is_equal)
+        tt(B("pv", 256, 512), B("oh"), B("nmd"), A.mult)
+        scan(B("wb"), B("r01"), B("pv", 256, 512), A.mult, A.add)
+        ts(starts("zz"), ends("wb"), 1.0, A.add)
+        bcast(B("tmp1"))
+        for q in range(2):
+            mm(B("pz", 128 * q, 128 * q + 128), B("tmp1", 128 * q, 128 * q + 128), B("idf"), True, True)
+        ts(si(0), ends("km"), 512.0, A.mult)
+        ts(si(1), si(0), 15, A.bitwise_and)
+        ts(sm(6), ends("km"), (t + 1) / 32.0, A.is_lt)
+        ts(sm(7), ends("km"), 31.0 / 32, A.is_lt)
+        ts(sm(8), si(1), 8192.0, A.mult)
+        ts(sm(9), sm(6), 131072.0, A.mult)
+        ts(sm(10), sm(7), 262144.0, A.mult)
+        tt(sm(8), sm(8), ends("wb"), A.add)
+        tt(sm(9), sm(9), sm(10), A.add)
+        tt(starts("zz"), sm(8), sm(9), A.add)
+        bcast(B("pv", 0, 256))
+        tt(B("wm"), B("pv", 0, 256), B("dm"), A.mult)
+        to_lists(B("pz", 256, 272), "wm")
+        cp(B("pbu"), B("pz", 0, 256))
+        tt(B("pbm"), B("pz", 0, 256), B("tri"), A.mult)
+        cp(si(2), B("pz", 256, 272))
+        ts(si(3), si(2), 8191, A.bitwise_and)
+        ts(si(4), si(2), 13, A.arith_shift_right, 15, A.bitwise_and)
+        ts(si(5), si(2), 17, A.arith_shift_right, 1, A.bitwise_and)
+        ts(si(6), si(2), 18, A.arith_shift_right, 1, A.bitwise_and)
+        ts(sm(11), si(4), 256.0, A.mult)
+        tt(sm(11), sm(11), sm(5), A.add)
+        cp(B("l2"), sm(11))
+        ts(sm(12), si(3), 2.0, A.add)
+        tt(sm(13), si(3), sm(1), A.subtract)
+
+    for t in range(STEPS):
+        h, hn = B("hb%d" % (t % 2)), B("hb%d" % ((t + 1) % 2))
+        ts(B("pv", 0, 256), B("dk"), 31.0 / 32, A.is_ge, -128.0, A.mult)
+        tt(B("r1", 0, 256, 2), B("pv", 0, 256, 2), B("hid", 0, 256, 2), A.add)
+        tt(B("r2", 0, 256, 2), B("pv", 1, 256, 2), B("hid", 1, 256, 2), A.add)
+        for q in range(2):
+            mm(B("pk", 0, 128, 1, 0, 48), B("we", 48 * q, 48 * q + 48), B(h[0], 128 * q, 128 * q + 128), q == 0, q == 1)
+        for q in range(2):
+            mm(B("ps", 128 * q, 128 * q + 128), B("r1", 128 * q, 128 * q + 128), B("idb"), True, True)
+        for q in range(2):
+            mm(B("ps", 256 + 128 * q, 384 + 128 * q), B("r2", 128 * q, 128 * q + 128), B("idb"), True, True)
+        act(B("r1a"), B("ps", 0, 256), AF.Copy)
+        act(B("r2a"), B("ps", 256, 512), AF.Copy)
+        u48 = B("ui", 0, 128, 1, 0, 48)
+        cp(u48, B("pk", 0, 128, 1, 0, 48))
+        m48 = B("um", 0, 128, 1, 0, 48)
+        ts(m48, u48, 4095, A.bitwise_and)
+        hi16 = B("um", 0, 128, 1, 32, 48)
+        q16 = B("usq", 0, 128, 1, 32, 48)
+        s16 = B("ui", 0, 128, 1, 32, 48)
+        tt(q16, hi16, hi16, A.mult)
+        cp(B("rz", 0, 128, 1, 0, 16), B("um", 0, 128, 1, 0, 16))
+        ts(s16, q16, 4, A.arith_shift_right)
+        ts(B("rz", 0, 128, 1, 32, 48), s16, B("acol", 0, 1, 1, 32, 48), A.add)
+        rz = B("rz", 0, 128, 1, 0, 48)
+        for q in range(2):
+            mm(B("pz", 128 * q, 128 * q + 128), B("lzo", 128 * q, 128 * q + 128, 1, 0, 48), rz, True, True)
+        for q in range(2):
+            o = B("pz", 256 + 128 * q, 384 + 128 * q)
+            mm(o, B("nmo", 128 * q, 128 * q + 128), B("idf"), True, False)
+            mm(o, B("lze", 128 * q, 128 * q + 128, 1, 0, 48), rz, False, True)
+
+        def names(j):
+            for z in range(2):
+                s = 2 * j + z
+                mm(B(("pa", "pb", "pc")[j % 3], 256 * z, 256 * z + 256), B("bs", 128 * j, 128 * j + 128), B(("r1a", "r2a")[z]), True, True)
+        for j in range(3):
+            names(j)
+        cp(B("zi"), B("pz", 0, 256))
+        ts(B("bit"), B("zi"), 3, A.arith_shift_right, 1, A.bitwise_and)
+        tt(B("mz"), B("bit"), B("pz", 0, 256), A.mult)
+        tt(B("a0"), B("mz"), B("pz", 256, 512), A.add)
+        ts(B("ai"), B("a0"), 8191, A.bitwise_and)
+        mm(B("py", 0, 256), B("onesb", 0, 128, 1, 0, 2), B("cy", 0, 256, 1, 0, 2), True, False)
+        for j in range(8):
+            for z in range(2):
+                s = 2 * j + z
+                tt(B("eqb", 256 * s, 256 * s + 256), B(("pa", "pb", "pc")[j % 3], 256 * z, 256 * z + 256), B("ai"), A.is_equal)
+            if j + 3 < 8:
+                names(j + 3)
+            for z in range(2):
+                s = 2 * j + z
+                mm(B("py", 0, 256), B("wh", 128 * s, 128 * s + 128), B("eqb", 256 * s, 256 * s + 256), False, s == S - 1)
+        tt(B("off"), B("py", 0, 256), B("ai"), A.max)
+        cp(B("ou", HALF, 256), B("off", HALF, 256))
+        cp(B("ou", 0, HALF), B("off", 0, HALF))
+        for q in range(2):
+            o = B("py", 256 + 128 * q, 384 + 128 * q)
+            mm(o, B("onesb", 0, 128, 1, 0, 1), B("ck16", 0, 128, 1, 0, 1), True, False)
+            mm(o, B("off", 128 * q, 128 * q + 128), B("idf"), False, True)
+        if t == 0:
+            early_drain(t)
+            n_ag = sum(arrives(c) for c in T.cores if c != core)
+            wait("v", "ag", n_ag)
+            wait("s", "ag", n_ag)
+        else:
+            scatter_all(t - 1)
+        e1 = 16 * HALF
+        op("v", lambda: g.vector.tensor_tensor(T.xs[:, 0:e1], ap(win).indirect(T.ou[:, 0:HALF]), T.hexp[:, 0:e1], A.subtract),
+           [B("xs", 0, e1)], [win, B("ou", 0, HALF), B("hexp", 0, e1)])
+        for z in range(2):
+            c0, c1 = HALF + (256 - HALF) // 2 * z, HALF + (256 - HALF) // 2 * (z + 1)
+            op("s", lambda: g.scalar.activation(T.xs[:, 16 * c0:16 * c1], ap(win).indirect(T.ou[:, c0:c1]), AF.Copy),
+               [B("xs", 16 * c0, 16 * c1)], [win, B("ou", c0, c1)])
+        act(B("ab", 0, e1), B("xs", 0, e1), AF.Abs)
+        for b in range(4):
+            c0 = e1 + 512 * b
+            bank = B(("pa", "pb", "pc")[b % 3])
+            mm(bank, B("idb"), B("xs", c0, c0 + 512), True, False)
+            mm(bank, B("nidb"), B("hexp", c0, c0 + 512), False, True)
+            act(B("ab", c0, c0 + 512), bank, AF.Abs)
+        for q in range(2):
+            mm(B("pk", 128 * q, 128 * q + 128), B("onesb", 0, 128, 1, 0, 1), B("ckf", 0, 128, 1, 0, 1), True, False)
+            for k in range(S):
+                mm(B("pk", 128 * q + k, 128 * q + 128, 16), B("ab", 2048 * q + k, 2048 * q + 2048, 16), B("gib"), False, k == S - 1)
+        for q in range(2):
+            scan(B("hs", 2048 * q, 2048 * q + 2048), B("rstn"), B("xs", 2048 * q, 2048 * q + 2048), A.add, A.max)
+            scan(B("lsc", 2048 * q, 2048 * q + 2048), B("rstp"), B("xs", 2048 * q, 2048 * q + 2048), A.add, A.min)
+        for q in range(2):
+            hq, lq = B("hs", 2048 * q + 15, 2048 * q + 2048, 16), B("lsc", 2048 * q + 15, 2048 * q + 2048, 16)
+            mm(B("ps", 8 * q, 8 * q + 8), hq, B("gib"), True, False)
+            mm(B("ps", 8 * q, 8 * q + 8), lq, B("ngib"), False, True)
+            s2 = B("pb", 128 * q, 128 * q + 128)
+            mm(s2, B("idb"), hq, True, False)
+            mm(s2, B("idb"), lq, False, q == 0)
+            if q == 1:
+                mm(s2, B("n2idb"), B(h[0], 128, 256), False, True)
+        act(B("yd"), B("pb", 0, 256), AF.Identity, 191.875, 0.5)
+        for q in range(2):
+            o = B("pc", 128 * q, 128 * q + 128)
+            mm(o, B("idb"), B("yd", 128 * q, 128 * q + 128), True, False)
+            mm(o, B("idb"), B(h[0], 128 * q, 128 * q + 128), False, True)
+            o = B("ps", 16 + 8 * q, 24 + 8 * q)
+            mm(o, B("yd", 128 * q, 128 * q + 128), B("gib"), True, False)
+            mm(o, B(h[0], 128 * q, 128 * q + 128), B("gib"), False, True)
+        act(B("yb"), B("pc", 0, 256), AF.Identity, -192.0)
+        act(hn, B("yd"), AF.Abs, -192.0)
+        if t > 0:
+            early_drain(t)
+        scan(B("km2"), B("r01"), B("pk", 0, 256), A.mult, A.max)
+        tt(B("rec"), B("pk", 0, 256), B("km2"), A.is_equal)
+        tt(B("ro"), B("py", 256, 512), B("rec"), A.mult)
+        scan(B("os"), B("r01"), B("ro"), A.mult, A.max)
+        tt(sm(14), B("ps", 0, 16), B("thd"), A.is_ge)
+        cp(si(7), ends("os"))
+        ts(sm(15), sm(14), 1.0 * DUM, A.mult)
+        ts(si(8), si(7), 16383, A.bitwise_and)
+        tt(sm(16), si(8), sm(15), A.max)
+        cp(starts("zz"), sm(16))
+        bcast(B("pv", 0, 256))
+        tt(B("wm"), B("pv", 0, 256), B("dm"), A.mult)
+        to_lists(B("ps", 32, 48), "wm")
+        w = sm(17)
+        cp(w, B("ps", 32, 48))
+        tt(sm(18), w, sm(2 + t), A.subtract)
+        ts(sm(19), w, 1.0 * VAL, A.is_ge)
+        ts(sm(20), w, 1.0 * DUM, A.is_ge)
+        tt(sm(21), sm(18), sm(19), A.mult)
+        tt(sm(22), sm(20), sm(0), A.mult)
+        tt(sm(23), sm(21), sm(2 + t), A.add)
+        tt(sm(24), sm(23), sm(22), A.add)
+        cp(B("stl"), sm(24))
+        op("v", lambda: g.vector.tensor_copy(ap(win).indirect(T.stl[:]), T.yb[:]), [win], [B("stl"), B("yb")])
+        lv, ln = B("lv%d" % t, TH * rank, TH * rank + TH), B("ln%d" % t, 16 * rank, 16 * rank + 16)
+        op("v", lambda: g.vector.tensor_copy(ap(lv), ap(win).indirect(T.l2[:])), [lv], [win, B("l2")])
+        send(lv, "x%d_%d" % (t, rank), "lv_%d" % t)
+        tt(sm(25), si(6), sm(20), A.mult)
+        tt(sm(26), si(5), sm(25), A.max)
+        tt(sm(27), sm(12), sm(26), A.mult)
+        ts(sm(28), sm(27), -1.0, A.add)
+        cp(starts("zc"), sm(28))
+        scan(B("pv", 0, 256), B("r01"), B("zc"), A.mult, A.add)
+        eb = B("eb", 0, 256)
+        tt(eb, B("pv", 0, 256), B("pbm"), A.is_equal)
+        mm(B("pz", 0, 256), B("bob"), eb, True, False)
+        e0 = 256
+        for c in range(15):
+            n = 256 - 16 * (c + 1)
+            eb = B("eb", e0, e0 + n)
+            e0 += n
+            ts(eb, B("pbu", 256 - n, 256), B("sm", 16 * 28 + c, 16 * 28 + c + 1), A.is_equal)
+            mm(B("pz", 256 - n, 256), B("bob"), eb, False, c == 14)
+        tt(B("pv", 256, 512), B("pz", 0, 256), B("dm"), A.mult)
+        scan(B("dsc"), B("r01"), B("pv", 256, 512), A.mult, A.add)
+        ts(sm(29), ends("dsc"), 0.5, A.is_lt)
+        tt(sm(30), sm(29), sm(26), A.mult)
+        tt(sm(31), sm(30), sm(13), A.mult)
+        tt(sm(32), sm(31), sm(1), A.add)
+        cp(ln, sm(32))
+        send(ln, "x%d_%d" % (t, rank), "ln_%d" % t)
+        if t + 1 < STEPS:
+            spread_h(hn)
+        tt(sm(33), sm(7), sm(14), A.mult)
+        tt(starts("zz"), sm(6), sm(33), A.max)
+        bcast(B("pv", 0, 256))
+        tt(B("tmp2"), B("pv", 0, 256), B("oh"), A.mult)
+        tt(B("dk"), B("dk"), B("tmp2"), A.add)
+        ts(sm(34), sm(16), 1.0 * VAL, A.is_lt)
+        cp(si(9), B("ps", 16, 32))
+        ts(si(10), si(9), 1, A.bitwise_and)
+        ts(sm(35), si(10), 1.0 / 32, A.mult, (t - 30) / 32.0, A.add)
+        tt(sm(35), sm(35), sm(34), A.mult)
+        dt_, nt_ = B("dk", t, 256, 16), B("nmd", t, 256, 16)
+        tt(dt_, dt_, sm(35), A.add)
+        tt(sm(36), sm(16), nt_, A.subtract)
+        tt(sm(36), sm(36), sm(34), A.mult)
+        tt(nt_, nt_, sm(36), A.add)
+        if t + 1 < STEPS:
+            cp(si(11), nt_)
+            ts(si(12), si(11), 7, A.arith_shift_right)
+            ts(si(13), si(11), 127, A.bitwise_and)
+            cp(B("hid", t, 256, 16), si(12))
+            if t % 2 == 0:
+                cp(B("r1", t + 1, 256, 16), si(13))
+            else:
+                cp(B("r2", t, 256, 16), si(13))
+                cp(B("nmo", t, 256, 16), nt_)
+            ac = B("acol", 1, 2)
+            op("v", lambda: g.vector.tensor_reduce(ap(ac), ap(sm(14)), AxisListType.X, A.add), [ac], [sm(14)])
+            mm(B("ps", 48, 49), B("onesf"), ac, True, True)
+            cp(B("coli", 2, 3), B("ps", 48, 49))
+            ts(B("coli", 3, 4), B("coli", 2, 3), 63, A.bitwise_and)
+            cp(B("acol", 0, 1), B("coli", 3, 4))
+    hl = "hb%d" % (STEPS % 2)
+    dma("y", T.yh[:], T[hl][:], [], [B(hl)])
+    ts(B("zi"), B("dk"), 512.0, A.mult)
+    ts(B("bit"), B("zi"), 4, A.arith_shift_right)
+    ts(B("tmp1"), B("bit"), 31.0, A.min)
+    for q in range(2):
+        mm(B("ps", 128 * q, 128 * q + 128), B("nmd", 128 * q, 128 * q + 128), B("idf"), True, True)
+        mm(B("ps", 256 + 128 * q, 384 + 128 * q), B("tmp1", 128 * q, 128 * q + 128), B("idf"), True, True)
+    act(B("onm"), B("ps", 0, 256), AF.Copy)
+    act(B("odu"), B("ps", 256, 512), AF.Copy)
+    dma("y", T.ypnd[:], T.onm[:], [], [B("onm")])
+    dma("y", T.ydue[:], T.odu[:], [], [B("odu")])
+    for s in range(S):
+        act(B("vali", s, 4096, 16), B("win", VAL + TH * s, VAL + TH * s + TH), AF.Copy)
+    dma("s", T.yval[:], T.vali[:], [], [B("vali")])
+    scatter_all(STEPS - 1)
+    dma("y", T.ymem[:], ap(own), [], [own])
+    for sem in sorted(held):
+        wait("g", sem, held[sem])

@@ -3,13 +3,18 @@ from concourse.mybir import dt, AluOpType as A, AxisListType, ActivationFunction
 
 N, C, TH, S, STEPS = 8, 1024, 256, 16, 3
 PL = N * C
-VAL = PL
-DUM = PL + S * TH
+VAL = PL + TH
+DUM = VAL + S * TH
 WC = DUM + TH
-HALF = 128
+UP = 64.0
+PARTS = (("v", 0, 64), ("s", 128, 192), ("v", 64, 128), ("s", 192, 256))
+ORDER = [0, 4, 1, 5, 2, 6, 3, 7]
+WAKE = 0.1
 
 SCRATCH = {
-    "win": ("sbuf", [128, WC], "bfloat16"),
+    "win": ("sbuf", [128, WC], "float32"), "winb": ("sbuf", [128, WC], "bfloat16"), "lvf": ("sbuf", [128, N * TH], "float32"),
+    "zz0": ("sbuf", [128, 256], "float32"), "zz1": ("sbuf", [128, 256], "float32"), "zz2": ("sbuf", [128, 256], "float32"),
+    "zz3": ("sbuf", [128, 256], "float32"), "zz4": ("sbuf", [128, 256], "float32"), "wm2": ("sbuf", [128, 256], "float32"),
     "vali": ("sbuf", [128, 4096], "bfloat16"),
     "hexp": ("sbuf", [128, 4096], "bfloat16"), "xs": ("sbuf", [128, 4096], "bfloat16"), "ab": ("sbuf", [128, 4096], "bfloat16"),
     "hs": ("sbuf", [128, 4096], "bfloat16"), "lsc": ("sbuf", [128, 4096], "bfloat16"), "eqb": ("sbuf", [128, 4096], "bfloat16"),
@@ -37,7 +42,7 @@ SCRATCH = {
     "rz": ("sbuf", [128, 128], "float32"), "zi": ("sbuf", [128, 256], "int32"), "bit": ("sbuf", [128, 256], "int32"),
     "mz": ("sbuf", [128, 256], "float32"), "a0": ("sbuf", [128, 256], "int32"), "ai": ("sbuf", [128, 256], "int32"),
     "off": ("sbuf", [128, 256], "float32"), "ou": ("sbuf", [128, 256], "uint16"),
-    "km": ("sbuf", [128, 256], "float32"), "zz": ("sbuf", [128, 256], "float32"), "oh": ("sbuf", [128, 256], "float32"),
+    "km": ("sbuf", [128, 256], "float32"), "oh": ("sbuf", [128, 256], "float32"),
     "wb": ("sbuf", [128, 256], "float32"), "wm": ("sbuf", [128, 256], "float32"),
     "pbu": ("sbuf", [128, 256], "uint16"), "pbm": ("sbuf", [128, 256], "float32"),
     "km2": ("sbuf", [128, 256], "float32"), "rec": ("sbuf", [128, 256], "float32"), "ro": ("sbuf", [128, 256], "float32"),
@@ -66,12 +71,9 @@ def rank_program(g, core, T, topo):
         return
     Q = {"v": g.vector, "s": g.scalar, "p": g.tensor, "g": g, "y": g.sync}
     SEM = {"v": "sv", "s": "ss", "p": "sp", "g": "sg"}
-    cnt = {q: 0 for q in Q}
-    clock = {q: {} for q in Q}
-    snap = {}
+    ops = []
     hist = {}
     ndma = [0]
-    held = {}
 
     def B(name, c0=0, c1=None, step=1, p0=0, p1=128):
         if c1 is None:
@@ -83,93 +85,166 @@ def rank_program(g, core, T, topo):
             return T[b[0]][b[1]:b[2], b[3]:b[4]]
         return T[b[0]][b[1]:b[2], b[3]:b[4]:b[5]]
 
-    def wait(q, sem, val):
-        if clock[q].get(sem, 0) >= val:
-            return
-        Q[q].wait_ge(T.sem[sem], val)
-        for k, v in snap.get((sem, val), {}).items():
-            if clock[q].get(k, 0) < v:
-                clock[q][k] = v
-        clock[q][sem] = val
-
-    def deps(q, outs, ins):
-        need = {}
+    def record(q, kind, fn, outs, ins, cost, lat, tok=None, pre=(), after=()):
+        me = len(ops)
+        preds = {}
         for b, w in [(o, True) for o in outs] + [(i, False) for i in ins]:
             bank = b[0] in PSUM
-            for (c0, c1, hw, hq, tok, st) in hist.get(b[0], []):
-                if not bank and (c1 <= b[3] or b[4] <= c0):
+            for (c0, c1, hw, i, st) in hist.get(b[0], []):
+                hq, hk = ops[i]["q"], ops[i]["kind"]
+                apart = c1 <= b[3] or b[4] <= c0 or (st == b[5] and (c0 - b[3]) % st != 0)
+                same = hq == q and hk == "c" and kind == "c"
+                if bank and q == "p" and hq == "p":
+                    preds.setdefault(i, False)
                     continue
-                if not bank and st == b[5] and (c0 - b[3]) % st:
+                if apart and not (bank and not same):
                     continue
-                if not (w or hw) and not (bank and hq != q):
+                if not (w or hw) and not (bank and not same):
                     continue
-                if hq == q and q != "y":
-                    if not hw or q == "p":
-                        continue
-                    if bank and (c1 <= b[3] or b[4] <= c0):
-                        continue
-                if need.get(tok[0], 0) < tok[1]:
-                    need[tok[0]] = tok[1]
-        for sem in sorted(need):
-            wait(q, sem, need[sem])
-
-    def note(q, outs, ins, tok):
-        snap[tok] = dict(clock[q])
-        held[tok[0]] = tok[1]
+                preds[i] = True
+        ops.append({"q": q, "kind": kind, "fn": fn, "preds": preds, "cost": cost, "lat": lat, "tok": tok, "pre": list(pre), "after": list(after)})
         for b, w in [(o, True) for o in outs] + [(i, False) for i in ins]:
-            h = hist.setdefault(b[0], [])
             keep = []
-            for e in h:
-                if w and b[5] == 1 and b[2] - b[1] == 128 and b[3] <= e[0] and e[1] <= b[4] and b[0] not in PSUM and not (e[3] == "y"):
+            for e in hist.get(b[0], []):
+                if w and b[5] == 1 and b[2] - b[1] == 128 and b[3] <= e[0] and e[1] <= b[4] and b[0] not in PSUM:
                     continue
-                if e[3] == q and q in SEM and e[2] == w and e[0] == b[3] and e[1] == b[4] and e[5] == b[5]:
+                if b[0] in PSUM and e[2] == w and ops[e[3]]["q"] == q and e[0] == b[3] and e[1] == b[4] and e[4] == b[5] and (w and q == "p"):
                     continue
                 keep.append(e)
-            keep.append((b[3], b[4], w, q, tok, b[5]))
+            keep.append((b[3], b[4], w, me, b[5]))
             hist[b[0]] = keep
+        return me
 
-    def op(q, fn, outs, ins):
-        deps(q, outs, ins)
-        cnt[q] += 1
-        fn().then_inc(T.sem[SEM[q]], 1)
-        note(q, outs, ins, (SEM[q], cnt[q]))
+    def op(q, fn, outs, ins, cost, pre=(), after=()):
+        return record(q, "c", fn, outs, ins, cost, WAKE, None, pre, after)
 
-    def dma(q, out, in_, outs, ins):
-        deps(q, outs, ins)
+    def dma(q, out, in_, outs, ins, nbytes):
         sem = "d%d" % ndma[0]
         ndma[0] += 1
-        Q[q].dma_start(out, in_).then_inc(T.sem[sem], 16)
-        note("y", outs, ins, (sem, 16))
+        return record(q, "d", lambda: Q[q].dma_start(out, in_), outs, ins, 0.1, 2.0 + nbytes / 2e5, (sem, 16))
+
+    def emit():
+        n = len(ops)
+        succ = [[] for _ in range(n)]
+        left = [0] * n
+        for j in range(n):
+            es = [(i, ops[i]["lat"] if w else 0.0) for i, w in ops[j]["preds"].items()] + ops[j]["after"]
+            left[j] = len(es)
+            for i, l in es:
+                succ[i].append((j, l))
+        prio = [0.0] * n
+        for i in range(n - 1, -1, -1):
+            prio[i] = ops[i]["cost"] + max([prio[j] + l for j, l in succ[i]] + [ops[i]["lat"] if ops[i]["kind"] == "d" else 0.0])
+        rdy = [0.0] * n
+        cand = {q: [i for i in range(n) if not left[i] and ops[i]["q"] == q] for q in Q}
+        free = {q: 0.0 for q in Q}
+        order = []
+        while len(order) < n:
+            best = None
+            for q in Q:
+                if not cand[q]:
+                    continue
+                e0 = max(free[q], min(rdy[i] for i in cand[q]))
+                i = max([i for i in cand[q] if rdy[i] <= e0 + 1e-9], key=lambda i: (prio[i], -i))
+                if best is None or e0 < best[0]:
+                    best = (e0, q, i)
+            e0, q, i = best
+            cand[q].remove(i)
+            order.append(i)
+            free[q] = e0 + ops[i]["cost"]
+            for j, l in succ[i]:
+                rdy[j] = max(rdy[j], free[q] + l)
+                left[j] -= 1
+                if not left[j]:
+                    cand[ops[j]["q"]].append(j)
+        clock = {q: {} for q in Q}
+        snap, held = {}, {}
+        cnt = {q: 0 for q in Q}
+
+        def wait(q, sem, val):
+            if clock[q].get(sem, 0) >= val:
+                return
+            Q[q].wait_ge(T.sem[sem], val)
+            for k, v in snap.get((sem, val), {}).items():
+                if clock[q].get(k, 0) < v:
+                    clock[q][k] = v
+            clock[q][sem] = val
+
+        for i in order:
+            o = ops[i]
+            q = o["q"]
+            need = {}
+            for sem, val in o["pre"] + [ops[j]["tok"] for j, w in o["preds"].items() if w]:
+                need[sem] = max(need.get(sem, 0), val)
+            for sem in sorted(need):
+                wait(q, sem, need[sem])
+            r = o["fn"]()
+            if o["kind"] == "c":
+                cnt[q] += 1
+                o["tok"] = (SEM[q], cnt[q])
+                r.then_inc(T.sem[SEM[q]], 1)
+            elif o["kind"] == "d":
+                r.then_inc(T.sem[o["tok"][0]], 16)
+            snap[o["tok"]] = dict(clock[q])
+            held[o["tok"][0]] = max(held.get(o["tok"][0], 0), o["tok"][1])
+        for sem in sorted(held):
+            wait("g", sem, held[sem])
+
+    CYC = 0.001
+
+    def wd(b):
+        return (b[4] - b[3] + b[5] - 1) // b[5]
+
+    def two(*bs):
+        return all(SCRATCH[b[0]][2] in ("bfloat16", "uint16") for b in bs if wd(b) > 1)
 
     def cp(o, i):
-        op("v", lambda: g.vector.tensor_copy(ap(o), ap(i)), [o], [i])
+        op("v", lambda: g.vector.tensor_copy(ap(o), ap(i)), [o], [i], CYC * max(64, wd(o) * (0.5 if two(o, i) else 1)))
 
     def tt(o, a, b, f):
-        op("v", lambda: g.vector.tensor_tensor(ap(o), ap(a), ap(b), f), [o], [a, b])
+        op("v", lambda: g.vector.tensor_tensor(ap(o), ap(a), ap(b), f), [o], [a, b],
+           CYC * max(64, wd(o) * (1 if a[0] in PSUM or b[0] in PSUM else 2)))
 
     def ts(o, a, s1, f1, s2=None, f2=None):
         x1 = ap(s1) if isinstance(s1, tuple) else s1
         x2 = ap(s2) if isinstance(s2, tuple) else s2
         ins = [a] + [s for s in (s1, s2) if isinstance(s, tuple)]
+        c = CYC * max(64, wd(o) * (0.5 if two(o, a) else 1))
         if f2 is None:
-            op("v", lambda: g.vector.tensor_scalar(ap(o), ap(a), x1, None, f1), [o], ins)
+            op("v", lambda: g.vector.tensor_scalar(ap(o), ap(a), x1, None, f1), [o], ins, c)
         else:
-            op("v", lambda: g.vector.tensor_scalar(ap(o), ap(a), x1, x2, f1, f2), [o], ins)
+            op("v", lambda: g.vector.tensor_scalar(ap(o), ap(a), x1, x2, f1, f2), [o], ins, c)
 
     def fill(o, c):
-        op("v", lambda: g.vector.memset(ap(o), c), [o], [])
+        op("v", lambda: g.vector.memset(ap(o), c), [o], [], CYC * max(64, wd(o) * (0.5 if two(o) else 1)))
 
     def scan(o, d0, d1, f0, f1):
-        op("v", lambda: g.vector.tensor_tensor_scan(ap(o), ap(d0), ap(d1), 0.0, f0, f1), [o], [d0, d1])
+        op("v", lambda: g.vector.tensor_tensor_scan(ap(o), ap(d0), ap(d1), 0.0, f0, f1), [o], [d0, d1],
+           CYC * max(64, wd(o) * (0.5 if two(o, d0, d1) else 1)))
 
     def act(o, i, f, bias=0.0, scale=1.0):
-        op("s", lambda: g.scalar.activation(ap(o), ap(i), f, bias=bias, scale=scale), [o], [i])
+        op("s", lambda: g.scalar.activation(ap(o), ap(i), f, bias=bias, scale=scale), [o], [i], CYC * max(64, wd(o)))
 
     def mm(o, l, r, st, sp):
-        op("p", lambda: g.tensor.matmul(ap(o), ap(l), ap(r), st, sp), [o], [l, r])
+        op("p", lambda: g.tensor.matmul(ap(o), ap(l), ap(r), st, sp), [o], [l, r],
+           0.00085 * max(min(64, wd(l)), wd(r)) * (4 if SCRATCH[l[0]][2] == "float32" else 1))
 
     def iota(o, pat, base, cm):
-        op("g", lambda: g.iota(ap(o), pat, base, cm), [o], [])
+        op("g", lambda: g.iota(ap(o), pat, base, cm), [o], [], 0.2 + 2 * CYC * wd(o))
+
+    def gather(q, o, w, off, pre=(), after=()):
+        c = 0.06 + 1.5 * CYC * wd(o)
+        if q == "v":
+                op("v", lambda: g.vector.tensor_copy(ap(o), ap(w).indirect(ap(off))), [o], [w, off], c, pre, after)
+        else:
+            op("s", lambda: g.scalar.activation(ap(o), ap(w).indirect(ap(off)), AF.Copy), [o], [w, off], c, pre, after)
+
+    def scatter(q, w, off, i, pre=(), after=()):
+        c = 0.06 + 3.8 * CYC * wd(i)
+        if q == "v":
+            op("v", lambda: g.vector.tensor_copy(ap(w).indirect(ap(off)), ap(i)), [w], [off, i], c, pre, after)
+        else:
+            op("s", lambda: g.scalar.activation(ap(w).indirect(ap(off)), ap(i), AF.Silu), [w], [off, i], c, pre, after)
 
     def sm(k):
         return B("sm", 16 * k, 16 * k + 16)
@@ -183,16 +258,16 @@ def rank_program(g, core, T, topo):
     def starts(n):
         return B(n, 0, 256, 16)
 
-    win = B("win")
-    own = B("win", rank * C, rank * C + C)
+    win, winb, wval = B("win"), B("winb"), B("win", VAL, WC)
+    own, own_up = [B(n, rank * C, rank * C + C) for n in ("winb", "win")]
 
     def send(b, sem, loc):
         others = [c for c in T.cores if c != core]
+        nb = wd(b) * 256
         far = [c for c in others if topo.chip(c) != topo.chip(core)]
         near = [c for c in others if topo.chip(c) == topo.chip(core)]
         ef = topo.engines(core, far[0])
         en = [e for e in topo.engines(core, near[0]) if e not in ef]
-        deps("g", [], [b])
         trs = []
         for dst, eng in ((far, ef), (near, en)):
             ids = []
@@ -201,8 +276,8 @@ def rank_program(g, core, T, topo):
                 ids.append(DstId(rid=rid, pnc=pid))
             trs.append(RemoteDMATransfer(dst_ids=ids, dma_engine_mask=sum(1 << e for e in eng), remote_sem=T.sem[sem],
                                          srcs=[ap(b)], dsts=[ap(b)] * len(ids), alu_op=0))
-        g.remote_dma_fused(trs, local_sem=T.sem[loc])
-        note("y", [], [b], (loc, len(ef) + len(en)))
+        lat = 2.5 + nb / 2e4
+        return record("g", "r", lambda: g.remote_dma_fused(trs, local_sem=T.sem[loc]), [], [b], 1.0, lat, (loc, len(ef) + len(en))), lat
 
     def arrives(src):
         ef = topo.engines(src, [c for c in T.cores if topo.chip(c) != topo.chip(src)][0])
@@ -210,17 +285,17 @@ def rank_program(g, core, T, topo):
             return len(ef)
         return len([e for e in topo.engines(src, core) if e not in ef])
 
-    dma("y", ap(own), T.mem[:], [own], [])
-    dma("s", T.hb0[:], T.h[:], [B("hb0")], [])
-    dma("y", T.praw[:], T.pnd[:], [B("praw")], [])
-    dma("s", T.draw[:], T.due[:], [B("draw")], [])
-    dma("y", T.wraw[:, 0:1], T.w[:], [B("wraw")], [])
-    dma("s", T.kraw[:, 0:1], T.kap[:], [B("kraw")], [])
-    dma("y", T.traw[:, 0:1], T.th[:], [B("traw")], [])
-    dma("s", T.vali[:], T.val[:], [B("vali")], [])
+    dma("y", ap(own), T.mem[:], [own], [], 262144)
+    dma("s", T.hb0[:], T.h[:], [B("hb0")], [], 65536)
+    dma("y", T.praw[:], T.pnd[:], [B("praw")], [], 131072)
+    dma("s", T.draw[:], T.due[:], [B("draw")], [], 131072)
+    dma("y", T.wraw[:, 0:1], T.w[:], [B("wraw")], [], 512)
+    dma("s", T.kraw[:, 0:1], T.kap[:], [B("kraw")], [], 512)
+    dma("y", T.traw[:, 0:1], T.th[:], [B("traw")], [], 512)
+    dma("s", T.vali[:], T.val[:], [B("vali")], [], 1048576)
     iota(B("iotp", 0, 1), [[0, 1]], 0, 1)
     iota(B("iotc"), [[1, 256]], 0, 0)
-    send(own, "ag", "la")
+    ag = send(own, "ag", "la")
 
     PF, PG, PM, PS, WCOL, KCOL, TCOL = [B("colf", k, k + 1) for k in range(7)]
     cp(PF, B("iotp", 0, 1))
@@ -289,7 +364,7 @@ def rank_program(g, core, T, topo):
         ts(B("bs", 128 * q, 128 * q + 128), B("bob"), B("w8", 16 + q, 17 + q), A.mult)
     for s in range(S):
         ts(B("wh", 128 * s, 128 * s + 128), B("idb"), 256.0 * (64 + s), A.mult)
-    fill(B("cy", 0, 256, 1, 0, 2), -8192.0)
+    fill(B("cy", 0, 256, 1, 0, 2), VAL - 16384.0)
     cp(B("cy", 0, 256, 1, 0, 1), B("iotc", 0, 256, 1, 0, 1))
     ts(B("ckf", 0, 128, 1, 0, 1), B("cm", 0, 128, 1, 0, 1), -1.0 / 16, A.mult, 15.0 / 16, A.add)
     ts(B("ck16", 0, 128, 1, 0, 1), B("cm", 0, 128, 1, 0, 1), 16384.0, A.mult)
@@ -298,15 +373,15 @@ def rank_program(g, core, T, topo):
     ts(B("n2idb"), B("idb"), -2.0, A.mult)
     ts(B("ngib"), B("gib"), -1.0, A.mult)
     ts(sm(0), B("iotc", 0, 16), 16.0, A.mult, PM, A.add)
-    ts(sm(1), sm(0), 1.0 * DUM, A.add)
+    ts(sm(1), sm(0), 1.0 * PL, A.add)
     for t in range(STEPS):
         ts(sm(2 + t), sm(0), 1.0 * VAL + TH * t, A.add)
-    ts(sm(5), sm(0), 1.0 * VAL, A.add)
     fill(B("rstp"), 0.0)
     fill(B("rstn"), 0.0)
     fill(B("rstp", 0, 2048, 16), 256.0)
     fill(B("rstn", 0, 2048, 16), -256.0)
-    fill(B("zz"), 0.0)
+    for k in range(5):
+        fill(B("zz%d" % k), 0.0)
     fill(B("zc"), 0.0)
 
     def spread_h(h):
@@ -315,31 +390,37 @@ def rank_program(g, core, T, topo):
 
     spread_h(B("hb0"))
     for s in range(S):
-        act(B("win", VAL + TH * s, VAL + TH * s + TH), B("vali", s, 4096, 16), AF.Copy)
+        act(B("winb", VAL + TH * s, VAL + TH * s + TH), B("vali", s, 4096, 16), AF.Copy)
+    for s in range(S):
+        act(B("win", VAL + TH * s, VAL + TH * s + TH), B("vali", s, 4096, 16), AF.Identity, UP)
 
-    def bcast(dst):
-        scan(dst, B("r01"), B("zz"), A.mult, A.add)
+    def bcast(dst, k):
+        scan(dst, B("r01"), B("zz%d" % k), A.mult, A.add)
 
     def to_lists(dst, src_m):
         for q in range(2):
             mm(B(dst[0], dst[3] + 8 * q, dst[3] + 8 * q + 8), B(src_m, 128 * q, 128 * q + 128), B("gif"), True, True)
 
-    def scatter_all(t):
+    def scatter_all(t, sent):
         for r in range(N - 1, -1, -1):
             lv, ln = B("lv%d" % t, TH * r, TH * r + TH), B("ln%d" % t, 16 * r, 16 * r + 16)
-            if r != rank:
-                wait("v", "x%d_%d" % (t, r), 2 * arrives(T.cores[r]))
-            op("v", lambda: g.vector.tensor_copy(ap(win).indirect(ap(ln)), ap(lv)), [win], [lv, ln])
+            pre = [] if r == rank else [("x%d_%d" % (t, r), 2 * arrives(T.cores[r]))]
+            if t + 1 == STEPS:
+                scatter("v", B("winb", 0, VAL), ln, lv, pre, sent)
+            else:
+                lf = B("lvf", TH * r, TH * r + TH)
+                op("v", lambda o=lf, i=lv: g.vector.tensor_copy(ap(o), ap(i)), [lf], [lv], CYC * TH, pre, sent)
+                scatter("s", B("win", 0, VAL), ln, lf, pre, sent)
 
     def early_drain(t):
         scan(B("km"), B("rstp", 0, 256), B("dk"), A.add, A.min)
-        cp(starts("zz"), ends("km"))
-        bcast(B("pv", 0, 256))
+        cp(starts("zz0"), ends("km"))
+        bcast(B("pv", 0, 256), 0)
         tt(B("oh"), B("pv", 0, 256), B("dk"), A.is_equal)
         tt(B("pv", 256, 512), B("oh"), B("nmd"), A.mult)
         scan(B("wb"), B("r01"), B("pv", 256, 512), A.mult, A.add)
-        ts(starts("zz"), ends("wb"), 1.0, A.add)
-        bcast(B("tmp1"))
+        ts(starts("zz1"), ends("wb"), 1.0, A.add)
+        bcast(B("tmp1"), 1)
         for q in range(2):
             mm(B("pz", 128 * q, 128 * q + 128), B("tmp1", 128 * q, 128 * q + 128), B("idf"), True, True)
         ts(si(0), ends("km"), 512.0, A.mult)
@@ -351,8 +432,8 @@ def rank_program(g, core, T, topo):
         ts(sm(10), sm(7), 262144.0, A.mult)
         tt(sm(8), sm(8), ends("wb"), A.add)
         tt(sm(9), sm(9), sm(10), A.add)
-        tt(starts("zz"), sm(8), sm(9), A.add)
-        bcast(B("pv", 0, 256))
+        tt(starts("zz2"), sm(8), sm(9), A.add)
+        bcast(B("pv", 0, 256), 2)
         tt(B("wm"), B("pv", 0, 256), B("dm"), A.mult)
         to_lists(B("pz", 256, 272), "wm")
         cp(B("pbu"), B("pz", 0, 256))
@@ -363,7 +444,7 @@ def rank_program(g, core, T, topo):
         ts(si(5), si(2), 17, A.arith_shift_right, 1, A.bitwise_and)
         ts(si(6), si(2), 18, A.arith_shift_right, 1, A.bitwise_and)
         ts(sm(11), si(4), 256.0, A.mult)
-        tt(sm(11), sm(11), sm(5), A.add)
+        tt(sm(11), sm(11), sm(0), A.add)
         cp(B("l2"), sm(11))
         ts(sm(12), si(3), 2.0, A.add)
         tt(sm(13), si(3), sm(1), A.subtract)
@@ -422,33 +503,29 @@ def rank_program(g, core, T, topo):
                 s = 2 * j + z
                 mm(B("py", 0, 256), B("wh", 128 * s, 128 * s + 128), B("eqb", 256 * s, 256 * s + 256), False, s == S - 1)
         tt(B("off"), B("py", 0, 256), B("ai"), A.max)
-        cp(B("ou", HALF, 256), B("off", HALF, 256))
-        cp(B("ou", 0, HALF), B("off", 0, HALF))
+        cp(B("ou", 128, 256), B("off", 128, 256))
+        cp(B("ou", 0, 128), B("off", 0, 128))
         for q in range(2):
             o = B("py", 256 + 128 * q, 384 + 128 * q)
             mm(o, B("onesb", 0, 128, 1, 0, 1), B("ck16", 0, 128, 1, 0, 1), True, False)
             mm(o, B("off", 128 * q, 128 * q + 128), B("idf"), False, True)
+        early_drain(t)
+        pre, after, up = [], [], UP
+        src = win
         if t == 0:
-            early_drain(t)
-            n_ag = sum(arrives(c) for c in T.cores if c != core)
-            wait("v", "ag", n_ag)
-            wait("s", "ag", n_ag)
-        else:
-            scatter_all(t - 1)
-        e1 = 16 * HALF
-        op("v", lambda: g.vector.tensor_tensor(T.xs[:, 0:e1], ap(win).indirect(T.ou[:, 0:HALF]), T.hexp[:, 0:e1], A.subtract),
-           [B("xs", 0, e1)], [win, B("ou", 0, HALF), B("hexp", 0, e1)])
-        for z in range(2):
-            c0, c1 = HALF + (256 - HALF) // 2 * z, HALF + (256 - HALF) // 2 * (z + 1)
-            op("s", lambda: g.scalar.activation(T.xs[:, 16 * c0:16 * c1], ap(win).indirect(T.ou[:, c0:c1]), AF.Copy),
-               [B("xs", 16 * c0, 16 * c1)], [win, B("ou", c0, c1)])
-        act(B("ab", 0, e1), B("xs", 0, e1), AF.Abs)
-        for b in range(4):
-            c0 = e1 + 512 * b
-            bank = B(("pa", "pb", "pc")[b % 3])
+            pre, after, up, src = [("ag", sum(arrives(c) for c in T.cores if c != core))], [ag], 0.0, winb
+        for q, c0, c1 in PARTS:
+            gather(q, B("xs", 16 * c0, 16 * c1), src, B("ou", c0, c1), pre, after)
+        if t == 0:
+            for r in range(N):
+                o, i = B("win", C * r, C * r + C), B("winb", C * r, C * r + C)
+                op("s", lambda o=o, i=i: g.scalar.activation(ap(o), ap(i), AF.Identity, bias=UP, scale=1.0), [o], [i], CYC * C, pre, after)
+        for b in ORDER:
+            c0 = 512 * b
+            bank = B(("pa", "pb", "pc")[ORDER.index(b) % 3])
             mm(bank, B("idb"), B("xs", c0, c0 + 512), True, False)
             mm(bank, B("nidb"), B("hexp", c0, c0 + 512), False, True)
-            act(B("ab", c0, c0 + 512), bank, AF.Abs)
+            act(B("ab", c0, c0 + 512), bank, AF.Abs, -up)
         for q in range(2):
             mm(B("pk", 128 * q, 128 * q + 128), B("onesb", 0, 128, 1, 0, 1), B("ckf", 0, 128, 1, 0, 1), True, False)
             for k in range(S):
@@ -462,10 +539,9 @@ def rank_program(g, core, T, topo):
             mm(B("ps", 8 * q, 8 * q + 8), lq, B("ngib"), False, True)
             s2 = B("pb", 128 * q, 128 * q + 128)
             mm(s2, B("idb"), hq, True, False)
-            mm(s2, B("idb"), lq, False, q == 0)
-            if q == 1:
-                mm(s2, B("n2idb"), B(h[0], 128, 256), False, True)
-        act(B("yd"), B("pb", 0, 256), AF.Identity, 191.875, 0.5)
+            mm(s2, B("idb"), lq, False, False)
+            mm(s2, B("n2idb"), B(h[0], 128 * q, 128 * q + 128), False, True)
+        act(B("yd"), B("pb", 0, 256), AF.Identity, 191.875 - up, 0.5)
         for q in range(2):
             o = B("pc", 128 * q, 128 * q + 128)
             mm(o, B("idb"), B("yd", 128 * q, 128 * q + 128), True, False)
@@ -473,10 +549,8 @@ def rank_program(g, core, T, topo):
             o = B("ps", 16 + 8 * q, 24 + 8 * q)
             mm(o, B("yd", 128 * q, 128 * q + 128), B("gib"), True, False)
             mm(o, B(h[0], 128 * q, 128 * q + 128), B("gib"), False, True)
-        act(B("yb"), B("pc", 0, 256), AF.Identity, -192.0)
+        act(B("yb"), B("pc", 0, 256), AF.Identity, UP - 192.0)
         act(hn, B("yd"), AF.Abs, -192.0)
-        if t > 0:
-            early_drain(t)
         scan(B("km2"), B("r01"), B("pk", 0, 256), A.mult, A.max)
         tt(B("rec"), B("pk", 0, 256), B("km2"), A.is_equal)
         tt(B("ro"), B("py", 256, 512), B("rec"), A.mult)
@@ -486,10 +560,10 @@ def rank_program(g, core, T, topo):
         ts(sm(15), sm(14), 1.0 * DUM, A.mult)
         ts(si(8), si(7), 16383, A.bitwise_and)
         tt(sm(16), si(8), sm(15), A.max)
-        cp(starts("zz"), sm(16))
-        bcast(B("pv", 0, 256))
-        tt(B("wm"), B("pv", 0, 256), B("dm"), A.mult)
-        to_lists(B("ps", 32, 48), "wm")
+        cp(starts("zz3"), sm(16))
+        bcast(B("pv", 0, 256), 3)
+        tt(B("wm2"), B("pv", 0, 256), B("dm"), A.mult)
+        to_lists(B("ps", 32, 48), "wm2")
         w = sm(17)
         cp(w, B("ps", 32, 48))
         tt(sm(18), w, sm(2 + t), A.subtract)
@@ -499,11 +573,11 @@ def rank_program(g, core, T, topo):
         tt(sm(22), sm(20), sm(0), A.mult)
         tt(sm(23), sm(21), sm(2 + t), A.add)
         tt(sm(24), sm(23), sm(22), A.add)
-        cp(B("stl"), sm(24))
-        op("v", lambda: g.vector.tensor_copy(ap(win).indirect(T.stl[:]), T.yb[:]), [win], [B("stl"), B("yb")])
+        ts(B("stl"), sm(24), -1.0 * VAL, A.add)
+        scatter("v", wval, B("stl"), B("yb"))
         lv, ln = B("lv%d" % t, TH * rank, TH * rank + TH), B("ln%d" % t, 16 * rank, 16 * rank + 16)
-        op("v", lambda: g.vector.tensor_copy(ap(lv), ap(win).indirect(T.l2[:])), [lv], [win, B("l2")])
-        send(lv, "x%d_%d" % (t, rank), "lv_%d" % t)
+        gather("v", lv, wval, B("l2"))
+        sent = [send(lv, "x%d_%d" % (t, rank), "lv_%d" % t)]
         tt(sm(25), si(6), sm(20), A.mult)
         tt(sm(26), si(5), sm(25), A.max)
         tt(sm(27), sm(12), sm(26), A.mult)
@@ -527,12 +601,13 @@ def rank_program(g, core, T, topo):
         tt(sm(31), sm(30), sm(13), A.mult)
         tt(sm(32), sm(31), sm(1), A.add)
         cp(ln, sm(32))
-        send(ln, "x%d_%d" % (t, rank), "ln_%d" % t)
+        sent.append(send(ln, "x%d_%d" % (t, rank), "ln_%d" % t))
         if t + 1 < STEPS:
             spread_h(hn)
+            scatter_all(t, sent)
         tt(sm(33), sm(7), sm(14), A.mult)
-        tt(starts("zz"), sm(6), sm(33), A.max)
-        bcast(B("pv", 0, 256))
+        tt(starts("zz4"), sm(6), sm(33), A.max)
+        bcast(B("pv", 0, 256), 4)
         tt(B("tmp2"), B("pv", 0, 256), B("oh"), A.mult)
         tt(B("dk"), B("dk"), B("tmp2"), A.add)
         ts(sm(34), sm(16), 1.0 * VAL, A.is_lt)
@@ -556,13 +631,14 @@ def rank_program(g, core, T, topo):
                 cp(B("r2", t, 256, 16), si(13))
                 cp(B("nmo", t, 256, 16), nt_)
             ac = B("acol", 1, 2)
-            op("v", lambda: g.vector.tensor_reduce(ap(ac), ap(sm(14)), AxisListType.X, A.add), [ac], [sm(14)])
+            op("v", lambda ac=ac: g.vector.tensor_reduce(ap(ac), ap(sm(14)), AxisListType.X, A.add), [ac], [sm(14)], CYC * 64)
             mm(B("ps", 48, 49), B("onesf"), ac, True, True)
             cp(B("coli", 2, 3), B("ps", 48, 49))
             ts(B("coli", 3, 4), B("coli", 2, 3), 63, A.bitwise_and)
             cp(B("acol", 0, 1), B("coli", 3, 4))
     hl = "hb%d" % (STEPS % 2)
-    dma("y", T.yh[:], T[hl][:], [], [B(hl)])
+    act(B("winb", rank * C, rank * C + C), own_up, AF.Copy)
+    dma("y", T.yh[:], T[hl][:], [], [B(hl)], 65536)
     ts(B("zi"), B("dk"), 512.0, A.mult)
     ts(B("bit"), B("zi"), 4, A.arith_shift_right)
     ts(B("tmp1"), B("bit"), 31.0, A.min)
@@ -571,12 +647,12 @@ def rank_program(g, core, T, topo):
         mm(B("ps", 256 + 128 * q, 384 + 128 * q), B("tmp1", 128 * q, 128 * q + 128), B("idf"), True, True)
     act(B("onm"), B("ps", 0, 256), AF.Copy)
     act(B("odu"), B("ps", 256, 512), AF.Copy)
-    dma("y", T.ypnd[:], T.onm[:], [], [B("onm")])
-    dma("y", T.ydue[:], T.odu[:], [], [B("odu")])
+    dma("y", T.ypnd[:], T.onm[:], [], [B("onm")], 131072)
+    dma("y", T.ydue[:], T.odu[:], [], [B("odu")], 131072)
     for s in range(S):
-        act(B("vali", s, 4096, 16), B("win", VAL + TH * s, VAL + TH * s + TH), AF.Copy)
-    dma("s", T.yval[:], T.vali[:], [], [B("vali")])
-    scatter_all(STEPS - 1)
-    dma("y", T.ymem[:], ap(own), [], [own])
-    for sem in sorted(held):
-        wait("g", sem, held[sem])
+        act(B("vali", s, 4096, 16), B("win", VAL + TH * s, VAL + TH * s + TH), AF.Identity, -UP)
+    dma("s", T.yval[:], T.vali[:], [], [B("vali")], 1048576)
+    scatter_all(STEPS - 1, sent)
+    ts(B("ab", 0, C), own, -UP, A.add)
+    dma("y", T.ymem[:], T.ab[:, 0:C], [], [B("ab", 0, C)], 262144)
+    emit()

@@ -18,7 +18,7 @@ SCRATCH = {
     "vali": ("sbuf", [128, 4096], "bfloat16"),
     "hexp": ("sbuf", [128, 4096], "bfloat16"), "xs": ("sbuf", [128, 4096], "bfloat16"), "ab": ("sbuf", [128, 4096], "bfloat16"),
     "hs": ("sbuf", [128, 4096], "bfloat16"), "lsc": ("sbuf", [128, 4096], "bfloat16"), "eqb": ("sbuf", [128, 4096], "bfloat16"),
-    "rstn": ("sbuf", [128, 2048], "bfloat16"), "rstp": ("sbuf", [128, 2048], "bfloat16"),
+    "rstn": ("sbuf", [128, 1024], "bfloat16"), "rstp": ("sbuf", [128, 1024], "bfloat16"),
     "idb": ("sbuf", [128, 128], "bfloat16"), "nidb": ("sbuf", [128, 128], "bfloat16"), "n2idb": ("sbuf", [128, 128], "bfloat16"),
     "idf": ("sbuf", [128, 128], "float32"), "bob": ("sbuf", [128, 128], "bfloat16"),
     "gib": ("sbuf", [128, 8], "bfloat16"), "ngib": ("sbuf", [128, 8], "bfloat16"), "gif": ("sbuf", [128, 8], "float32"),
@@ -60,14 +60,70 @@ PSUM = ["pa", "pb", "pc", "pv", "pz", "py", "pk", "ps"]
 for _n in PSUM:
     SCRATCH[_n] = ("psum", [128, 512], "float32")
 NDMA = 16
-SEMAPHORES = ["sv", "ss", "sp", "sg", "ag", "la"] + ["d%d" % k for k in range(NDMA)]
-SEMAPHORES += [n + "_%d" % t for t in range(STEPS) for n in ("lv", "ln")]
-SEMAPHORES += ["x%d_%d" % (t, r) for t in range(STEPS) for r in range(N)]
+SEMAPHORES = ["sv", "ss", "sp", "sg", "ag1", "ag2", "agr", "hp", "la0", "la1", "la2", "lr0", "lr1"] + ["d%d" % k for k in range(NDMA)]
+SEMAPHORES += [n + "_%d" % t for t in range(STEPS) for n in ("lv", "ln")] + ["hv%d" % t for t in range(STEPS)]
+SEMAPHORES += [n + "%d_%d" % (t, r) for n in "xn" for t in range(STEPS) for r in range(N)]
+
+
+SPLIT = 576
+
+
+def chip_ranks(T, topo, core):
+    return [c for c in T.cores if topo.chip(c) == topo.chip(core)]
+
+
+def far_peers(T, topo, core):
+    k = chip_ranks(T, topo, core).index(core)
+    out = []
+    for c in T.cores:
+        if topo.chip(c) != topo.chip(core) and chip_ranks(T, topo, c).index(c) == k:
+            out.append(c)
+    return out
+
+
+def helper_of(T, topo, core):
+    k = chip_ranks(T, topo, core).index(core)
+    able = [c for c in topo.cores_of(core) if topo.die(c) != topo.die(core) and c not in T.cores
+            and all(topo.may_write(c, d) for d in T.cores if topo.chip(d) != topo.chip(core))]
+    return able[k]
+
+
+def helper_program(g, core, T, topo):
+    for c in T.cores:
+        if topo.chip(c) != topo.chip(core) or helper_of(T, topo, c) != core:
+            continue
+        r = T.rank_of(c)
+        peers = far_peers(T, topo, c)
+        sib = [d for d in chip_ranks(T, topo, c) if d != c][0]
+        came = [e for e in topo.engines(c, sib) if e not in topo.engines(c, peers[0])]
+        g.wait_ge(T.sem.hp, len(came))
+        b = T.winb[:, r * C + SPLIT:r * C + C]
+        ids = []
+        for d in peers:
+            rid, pid, _ = topo.addr(d)
+            ids.append(DstId(rid=rid, pnc=pid))
+        m = topo.mask(core, peers[0])
+        g.remote_dma_fused([RemoteDMATransfer(dst_ids=ids, dma_engine_mask=m, remote_sem=T.sem.ag2, srcs=[b], dsts=[b] * len(ids), alu_op=0)],
+                           local_sem=T.sem.la0)
+        far = [d for d in T.cores if topo.chip(d) != topo.chip(core)]
+        ids = []
+        for d in far:
+            rid, pid, _ = topo.addr(d)
+            ids.append(DstId(rid=rid, pnc=pid))
+        for t in range(STEPS):
+            b = T["lv%d" % t][:, TH * r + 128:TH * r + TH]
+            g.wait_ge(T.sem["hv%d" % t], len(came) // 2 - len(came) // 4)
+            g.remote_dma_fused([RemoteDMATransfer(dst_ids=ids, dma_engine_mask=m, remote_sem=T.sem["x%d_%d" % (t, r)], srcs=[b],
+                                                  dsts=[b] * len(ids), alu_op=0)], local_sem=T.sem["lv_%d" % t])
+        g.wait_ge(T.sem.la0, len(topo.engines(core, peers[0])))
+        for t in range(STEPS):
+            g.wait_ge(T.sem["lv_%d" % t], len(topo.engines(core, far[0])))
 
 
 def rank_program(g, core, T, topo):
     rank = T.rank_of(core)
     if rank is None:
+        helper_program(g, core, T, topo)
         return
     Q = {"v": g.vector, "s": g.scalar, "p": g.tensor, "g": g, "y": g.sync}
     SEM = {"v": "sv", "s": "ss", "p": "sp", "g": "sg"}
@@ -280,6 +336,8 @@ def rank_program(g, core, T, topo):
         return record("g", "r", lambda: g.remote_dma_fused(trs, local_sem=T.sem[loc]), [], [b], 1.0, lat, (loc, len(ef) + len(en))), lat
 
     def arrives(src):
+        if src == core:
+            return 0
         ef = topo.engines(src, [c for c in T.cores if topo.chip(c) != topo.chip(src)][0])
         if topo.chip(src) != topo.chip(core):
             return len(ef)
@@ -295,7 +353,39 @@ def rank_program(g, core, T, topo):
     dma("s", T.vali[:], T.val[:], [B("vali")], [], 1048576)
     iota(B("iotp", 0, 1), [[0, 1]], 0, 1)
     iota(B("iotc"), [[1, 256]], 0, 0)
-    ag = send(own, "ag", "la")
+    mates_, rows = chip_ranks(T, topo, core), [B("winb", r * C, r * C + C) for r in range(N)]
+    sib = [c for c in mates_ if c != core][0]
+    peers = far_peers(T, topo, core)
+    helper = helper_of(T, topo, core)
+    ef = topo.engines(core, peers[0])
+    en = [e for e in topo.engines(core, sib) if e not in ef]
+    lo, hi = B("winb", rank * C, rank * C + SPLIT), B("winb", rank * C + SPLIT, rank * C + C)
+
+    def transfer(dsts, eng, sem, b):
+        ids = []
+        for c in dsts:
+            rid, pid, _ = topo.addr(c)
+            ids.append(DstId(rid=rid, pnc=pid))
+        return RemoteDMATransfer(dst_ids=ids, dma_engine_mask=sum(1 << e for e in eng), remote_sem=T.sem[sem],
+                                 srcs=[ap(b)], dsts=[ap(b)] * len(ids), alu_op=0), len(eng)
+
+    def fused(trs, bs, loc, lat, pre=(), after=()):
+        count = sum(n for _, n in trs)
+        return record("g", "r", lambda: g.remote_dma_fused([x for x, _ in trs], local_sem=T.sem[loc]), [], bs, 1.0, lat, (loc, count), pre, after)
+
+    first = fused([transfer([helper], en, "hp", hi)], [hi], "la0", 3.0)
+    second = fused([transfer(peers, ef, "ag1", lo), transfer([sib], en, "agr", lo)], [lo], "la1", 8.0)
+    fused([transfer([sib], en, "agr", hi)], [hi], "la2", 3.0)
+    srcs = [T.rank_of(c) for c in peers]
+    ch = topo.engines(core, sib)
+    k4 = len(ch) // 4
+    got = [("ag1", len(ef) * len(peers)), ("ag2", len(ef) * len(peers))]
+    relays = []
+    for z in range(2):
+        bs = [B("winb", r * C + (0, SPLIT)[z], r * C + (SPLIT, C)[z]) for r in srcs]
+        trs = [transfer([sib], ch[k4 * x:k4 * x + k4], "agr", b) for x, b in enumerate(bs)]
+        relays.append((fused(trs, bs, "lr%d" % z, 3.5, [got[z]], [((second, 8.0), (first, 9.5))[z]]), 3.5))
+    got.append(("agr", 2 * len(en) + 2 * len(peers) * k4))
 
     PF, PG, PM, PS, WCOL, KCOL, TCOL = [B("colf", k, k + 1) for k in range(7)]
     cp(PF, B("iotp", 0, 1))
@@ -378,8 +468,8 @@ def rank_program(g, core, T, topo):
         ts(sm(2 + t), sm(0), 1.0 * VAL + TH * t, A.add)
     fill(B("rstp"), 0.0)
     fill(B("rstn"), 0.0)
-    fill(B("rstp", 0, 2048, 16), 256.0)
-    fill(B("rstn", 0, 2048, 16), -256.0)
+    fill(B("rstp", 0, 1024, 16), 256.0)
+    fill(B("rstn", 0, 1024, 16), -256.0)
     for k in range(5):
         fill(B("zz%d" % k), 0.0)
     fill(B("zc"), 0.0)
@@ -404,13 +494,14 @@ def rank_program(g, core, T, topo):
     def scatter_all(t, sent):
         for r in range(N - 1, -1, -1):
             lv, ln = B("lv%d" % t, TH * r, TH * r + TH), B("ln%d" % t, 16 * r, 16 * r + 16)
-            pre = [] if r == rank else [("x%d_%d" % (t, r), 2 * arrives(T.cores[r]))]
+            nv = 2 * len(ef) if topo.chip(T.cores[r]) != topo.chip(core) else len(en) // 2 + len(en) // 4
+            cv, cn = [[] if r == rank else [(n + "%d_%d" % (t, r), k)] for n, k in (("x", nv), ("n", arrives(T.cores[r])))]
             if t + 1 == STEPS:
-                scatter("v", B("winb", 0, VAL), ln, lv, pre, sent)
+                scatter("v", B("winb", 0, VAL), ln, lv, cv + cn, sent)
             else:
                 lf = B("lvf", TH * r, TH * r + TH)
-                op("v", lambda o=lf, i=lv: g.vector.tensor_copy(ap(o), ap(i)), [lf], [lv], CYC * TH, pre, sent)
-                scatter("s", B("win", 0, VAL), ln, lf, pre, sent)
+                op("v", lambda o=lf, i=lv: g.vector.tensor_copy(ap(o), ap(i)), [lf], [lv], CYC * TH, cv, sent[:1])
+                scatter("s", B("win", 0, VAL), ln, lf, cn, sent[1:])
 
     def early_drain(t):
         scan(B("km"), B("rstp", 0, 256), B("dk"), A.add, A.min)
@@ -513,7 +604,7 @@ def rank_program(g, core, T, topo):
         pre, after, up = [], [], UP
         src = win
         if t == 0:
-            pre, after, up, src = [("ag", sum(arrives(c) for c in T.cores if c != core))], [ag], 0.0, winb
+            pre, after, up, src = got, relays, 0.0, winb
         for q, c0, c1 in PARTS:
             gather(q, B("xs", 16 * c0, 16 * c1), src, B("ou", c0, c1), pre, after)
         if t == 0:
@@ -530,9 +621,9 @@ def rank_program(g, core, T, topo):
             mm(B("pk", 128 * q, 128 * q + 128), B("onesb", 0, 128, 1, 0, 1), B("ckf", 0, 128, 1, 0, 1), True, False)
             for k in range(S):
                 mm(B("pk", 128 * q + k, 128 * q + 128, 16), B("ab", 2048 * q + k, 2048 * q + 2048, 16), B("gib"), False, k == S - 1)
-        for q in range(2):
-            scan(B("hs", 2048 * q, 2048 * q + 2048), B("rstn"), B("xs", 2048 * q, 2048 * q + 2048), A.add, A.max)
-            scan(B("lsc", 2048 * q, 2048 * q + 2048), B("rstp"), B("xs", 2048 * q, 2048 * q + 2048), A.add, A.min)
+        for q in range(4):
+            scan(B("hs", 1024 * q, 1024 * q + 1024), B("rstn"), B("xs", 1024 * q, 1024 * q + 1024), A.add, A.max)
+            scan(B("lsc", 1024 * q, 1024 * q + 1024), B("rstp"), B("xs", 1024 * q, 1024 * q + 1024), A.add, A.min)
         for q in range(2):
             hq, lq = B("hs", 2048 * q + 15, 2048 * q + 2048, 16), B("lsc", 2048 * q + 15, 2048 * q + 2048, 16)
             mm(B("ps", 8 * q, 8 * q + 8), hq, B("gib"), True, False)
@@ -559,8 +650,8 @@ def rank_program(g, core, T, topo):
         cp(si(7), ends("os"))
         ts(sm(15), sm(14), 1.0 * DUM, A.mult)
         ts(si(8), si(7), 16383, A.bitwise_and)
-        tt(sm(16), si(8), sm(15), A.max)
-        cp(starts("zz3"), sm(16))
+        best = starts("zz3")
+        tt(best, si(8), sm(15), A.max)
         bcast(B("pv", 0, 256), 3)
         tt(B("wm2"), B("pv", 0, 256), B("dm"), A.mult)
         to_lists(B("ps", 32, 48), "wm2")
@@ -577,12 +668,17 @@ def rank_program(g, core, T, topo):
         scatter("v", wval, B("stl"), B("yb"))
         lv, ln = B("lv%d" % t, TH * rank, TH * rank + TH), B("ln%d" % t, 16 * rank, 16 * rank + 16)
         gather("v", lv, wval, B("l2"))
-        sent = [send(lv, "x%d_%d" % (t, rank), "lv_%d" % t)]
+        l0, l1 = B(lv[0], lv[3], lv[3] + 128), B(lv[0], lv[3] + 128, lv[4])
+        far = [c for c in T.cores if topo.chip(c) != topo.chip(core)]
+        xs = "x%d_%d" % (t, rank)
+        k2 = len(en) // 2
+        vt = [transfer(far, ef, xs, l0), transfer([sib], en[:k2], xs, l0), transfer([sib], en[k2:k2 + k2 // 2], xs, l1),
+              transfer([helper], en[k2 + k2 // 2:], "hv%d" % t, l1)]
+        sent = [(fused(vt, [l0, l1], "lv_%d" % t, 6.0), 6.0)]
         tt(sm(25), si(6), sm(20), A.mult)
         tt(sm(26), si(5), sm(25), A.max)
         tt(sm(27), sm(12), sm(26), A.mult)
-        ts(sm(28), sm(27), -1.0, A.add)
-        cp(starts("zc"), sm(28))
+        ts(starts("zc"), sm(27), -1.0, A.add)
         scan(B("pv", 0, 256), B("r01"), B("zc"), A.mult, A.add)
         eb = B("eb", 0, 256)
         tt(eb, B("pv", 0, 256), B("pbm"), A.is_equal)
@@ -592,7 +688,7 @@ def rank_program(g, core, T, topo):
             n = 256 - 16 * (c + 1)
             eb = B("eb", e0, e0 + n)
             e0 += n
-            ts(eb, B("pbu", 256 - n, 256), B("sm", 16 * 28 + c, 16 * 28 + c + 1), A.is_equal)
+            ts(eb, B("pbu", 256 - n, 256), B("zc", 16 * c, 16 * c + 1), A.is_equal)
             mm(B("pz", 256 - n, 256), B("bob"), eb, False, c == 14)
         tt(B("pv", 256, 512), B("pz", 0, 256), B("dm"), A.mult)
         scan(B("dsc"), B("r01"), B("pv", 256, 512), A.mult, A.add)
@@ -601,23 +697,23 @@ def rank_program(g, core, T, topo):
         tt(sm(31), sm(30), sm(13), A.mult)
         tt(sm(32), sm(31), sm(1), A.add)
         cp(ln, sm(32))
-        sent.append(send(ln, "x%d_%d" % (t, rank), "ln_%d" % t))
+        sent.append(send(ln, "n%d_%d" % (t, rank), "ln_%d" % t))
         if t + 1 < STEPS:
             spread_h(hn)
             scatter_all(t, sent)
         tt(sm(33), sm(7), sm(14), A.mult)
         tt(starts("zz4"), sm(6), sm(33), A.max)
         bcast(B("pv", 0, 256), 4)
-        tt(B("tmp2"), B("pv", 0, 256), B("oh"), A.mult)
-        tt(B("dk"), B("dk"), B("tmp2"), A.add)
-        ts(sm(34), sm(16), 1.0 * VAL, A.is_lt)
+        tt(B("pv", 256, 512), B("pv", 0, 256), B("oh"), A.mult)
+        tt(B("dk"), B("dk"), B("pv", 256, 512), A.add)
+        ts(sm(34), best, 1.0 * VAL, A.is_lt)
         cp(si(9), B("ps", 16, 32))
         ts(si(10), si(9), 1, A.bitwise_and)
         ts(sm(35), si(10), 1.0 / 32, A.mult, (t - 30) / 32.0, A.add)
         tt(sm(35), sm(35), sm(34), A.mult)
         dt_, nt_ = B("dk", t, 256, 16), B("nmd", t, 256, 16)
         tt(dt_, dt_, sm(35), A.add)
-        tt(sm(36), sm(16), nt_, A.subtract)
+        tt(sm(36), best, nt_, A.subtract)
         tt(sm(36), sm(36), sm(34), A.mult)
         tt(nt_, nt_, sm(36), A.add)
         if t + 1 < STEPS:

from concourse.bass import DstId, RemoteDMATransfer
from concourse.mybir import dt, AluOpType as A, AxisListType, ActivationFunctionType as AF

N, C, TH, S, STEPS = 8, 1024, 256, 16, 3
PL = N * C
VAL = PL + TH
DUM = VAL + S * TH
WC = DUM + TH
UP = 64.0
PARTS = (("v", 0, 64), ("s", 128, 192), ("v", 64, 128), ("s", 192, 256))
ORDER = [0, 4, 1, 5, 2, 6, 3, 7]
WAKE = 0.1

SCRATCH = {
    "win": ("sbuf", [128, WC], "float32"), "winb": ("sbuf", [128, WC], "bfloat16"), "lvf": ("sbuf", [128, N * TH], "float32"),
    "zz0": ("sbuf", [128, 256], "float32"), "zz1": ("sbuf", [128, 256], "float32"), "zz2": ("sbuf", [128, 256], "float32"),
    "zz3": ("sbuf", [128, 256], "float32"), "zz4": ("sbuf", [128, 256], "float32"), "wm2": ("sbuf", [128, 256], "float32"),
    "vali": ("sbuf", [128, 4096], "bfloat16"),
    "hexp": ("sbuf", [128, 4096], "bfloat16"), "xs": ("sbuf", [128, 4096], "bfloat16"), "ab": ("sbuf", [128, 4096], "bfloat16"),
    "hs": ("sbuf", [128, 4096], "bfloat16"), "lsc": ("sbuf", [128, 4096], "bfloat16"), "eqb": ("sbuf", [128, 4096], "bfloat16"),
    "rstn": ("sbuf", [128, 1024], "bfloat16"), "rstp": ("sbuf", [128, 1024], "bfloat16"),
    "idb": ("sbuf", [128, 128], "bfloat16"), "nidb": ("sbuf", [128, 128], "bfloat16"), "n2idb": ("sbuf", [128, 128], "bfloat16"),
    "idf": ("sbuf", [128, 128], "float32"), "bob": ("sbuf", [128, 128], "bfloat16"),
    "gib": ("sbuf", [128, 8], "bfloat16"), "ngib": ("sbuf", [128, 8], "bfloat16"), "gif": ("sbuf", [128, 8], "float32"),
    "bs": ("sbuf", [128, 1024], "bfloat16"), "wh": ("sbuf", [128, 2048], "bfloat16"),
    "onesb": ("sbuf", [128, 128], "bfloat16"), "onesf": ("sbuf", [128, 128], "float32"),
    "cy": ("sbuf", [128, 256], "bfloat16"), "ckf": ("sbuf", [128, 128], "bfloat16"), "ck16": ("sbuf", [128, 128], "bfloat16"),
    "we": ("sbuf", [128, 96], "bfloat16"), "lzo": ("sbuf", [128, 256], "float32"), "lze": ("sbuf", [128, 256], "float32"),
    "thd": ("sbuf", [128, 16], "float32"), "iotp": ("sbuf", [128, 8], "int32"), "iotc": ("sbuf", [128, 256], "int32"),
    "cg": ("sbuf", [128, 256], "int32"), "cm": ("sbuf", [128, 256], "int32"), "oc": ("sbuf", [128, 256], "float32"),
    "colf": ("sbuf", [128, 16], "float32"), "coli": ("sbuf", [128, 16], "int32"),
    "r01": ("sbuf", [128, 256], "float32"), "dm": ("sbuf", [128, 256], "float32"), "tri": ("sbuf", [128, 256], "float32"),
    "w8": ("sbuf", [128, 24], "float32"), "tmp1": ("sbuf", [128, 256], "float32"), "tmp2": ("sbuf", [128, 256], "float32"),
    "tmp3": ("sbuf", [128, 256], "float32"),
    "wraw": ("sbuf", [128, 8], "int32"), "kraw": ("sbuf", [128, 8], "int32"), "traw": ("sbuf", [128, 8], "int32"),
    "praw": ("sbuf", [128, 256], "int32"), "draw": ("sbuf", [128, 256], "int32"),
    "hb0": ("sbuf", [128, 256], "bfloat16"), "hb1": ("sbuf", [128, 256], "bfloat16"),
    "nmd": ("sbuf", [128, 256], "float32"), "nmo": ("sbuf", [128, 256], "float32"), "dk": ("sbuf", [128, 256], "float32"),
    "hid": ("sbuf", [128, 256], "float32"), "r1": ("sbuf", [128, 256], "bfloat16"), "r2": ("sbuf", [128, 256], "bfloat16"),
    "r1a": ("sbuf", [128, 256], "bfloat16"), "r2a": ("sbuf", [128, 256], "bfloat16"),
    "ui": ("sbuf", [128, 128], "int32"), "um": ("sbuf", [128, 128], "int32"), "usq": ("sbuf", [128, 128], "int32"),
    "rz": ("sbuf", [128, 128], "float32"), "zi": ("sbuf", [128, 256], "int32"), "bit": ("sbuf", [128, 256], "int32"),
    "mz": ("sbuf", [128, 256], "float32"), "a0": ("sbuf", [128, 256], "int32"), "ai": ("sbuf", [128, 256], "int32"),
    "off": ("sbuf", [128, 256], "float32"), "ou": ("sbuf", [128, 256], "uint16"),
    "km": ("sbuf", [128, 256], "float32"), "oh": ("sbuf", [128, 256], "float32"),
    "wb": ("sbuf", [128, 256], "float32"), "wm": ("sbuf", [128, 256], "float32"),
    "pbu": ("sbuf", [128, 256], "uint16"), "pbm": ("sbuf", [128, 256], "float32"),
    "km2": ("sbuf", [128, 256], "float32"), "rec": ("sbuf", [128, 256], "float32"), "ro": ("sbuf", [128, 256], "float32"),
    "os": ("sbuf", [128, 256], "float32"), "zc": ("sbuf", [128, 256], "float32"), "dsc": ("sbuf", [128, 256], "float32"),
    "sm": ("sbuf", [128, 640], "float32"), "si": ("sbuf", [128, 256], "int32"),
    "l2": ("sbuf", [128, 16], "uint16"), "stl": ("sbuf", [128, 16], "uint16"),
    "eb": ("sbuf", [128, 2304], "bfloat16"), "acol": ("sbuf", [128, 8], "float32"),
    "yd": ("sbuf", [128, 256], "bfloat16"), "yb": ("sbuf", [128, 256], "bfloat16"),
    "onm": ("sbuf", [128, 256], "float32"), "odu": ("sbuf", [128, 256], "float32"),
}
for _t in range(STEPS):
    SCRATCH["lv%d" % _t] = ("sbuf", [128, N * TH], "bfloat16")
    SCRATCH["ln%d" % _t] = ("sbuf", [128, N * 16], "uint16")
PSUM = ["pa", "pb", "pc", "pv", "pz", "py", "pk", "ps"]
for _n in PSUM:
    SCRATCH[_n] = ("psum", [128, 512], "float32")
NDMA = 16
SEMAPHORES = ["sv", "ss", "sp", "sg", "ag1", "ag2", "agr", "hp", "la0", "la1", "la2", "lr0", "lr1"] + ["d%d" % k for k in range(NDMA)]
SEMAPHORES += [n + "_%d" % t for t in range(STEPS) for n in ("lv", "ln")] + ["hv%d" % t for t in range(STEPS)]
SEMAPHORES += [n + "%d_%d" % (t, r) for n in "xn" for t in range(STEPS) for r in range(N)]


SPLIT = 576


def chip_ranks(T, topo, core):
    return [c for c in T.cores if topo.chip(c) == topo.chip(core)]


def far_peers(T, topo, core):
    k = chip_ranks(T, topo, core).index(core)
    out = []
    for c in T.cores:
        if topo.chip(c) != topo.chip(core) and chip_ranks(T, topo, c).index(c) == k:
            out.append(c)
    return out


def helper_of(T, topo, core):
    k = chip_ranks(T, topo, core).index(core)
    able = [c for c in topo.cores_of(core) if topo.die(c) != topo.die(core) and c not in T.cores
            and all(topo.may_write(c, d) for d in T.cores if topo.chip(d) != topo.chip(core))]
    return able[k]


def helper_program(g, core, T, topo):
    for c in T.cores:
        if topo.chip(c) != topo.chip(core) or helper_of(T, topo, c) != core:
            continue
        r = T.rank_of(c)
        peers = far_peers(T, topo, c)
        sib = [d for d in chip_ranks(T, topo, c) if d != c][0]
        came = [e for e in topo.engines(c, sib) if e not in topo.engines(c, peers[0])]
        g.wait_ge(T.sem.hp, len(came))
        b = T.winb[:, r * C + SPLIT:r * C + C]
        ids = []
        for d in peers:
            rid, pid, _ = topo.addr(d)
            ids.append(DstId(rid=rid, pnc=pid))
        m = topo.mask(core, peers[0])
        g.remote_dma_fused([RemoteDMATransfer(dst_ids=ids, dma_engine_mask=m, remote_sem=T.sem.ag2, srcs=[b], dsts=[b] * len(ids), alu_op=0)],
                           local_sem=T.sem.la0)
        far = [d for d in T.cores if topo.chip(d) != topo.chip(core)]
        ids = []
        for d in far:
            rid, pid, _ = topo.addr(d)
            ids.append(DstId(rid=rid, pnc=pid))
        for t in range(STEPS):
            b = T["lv%d" % t][:, TH * r + 128:TH * r + TH]
            g.wait_ge(T.sem["hv%d" % t], len(came) // 2 - len(came) // 4)
            g.remote_dma_fused([RemoteDMATransfer(dst_ids=ids, dma_engine_mask=m, remote_sem=T.sem["x%d_%d" % (t, r)], srcs=[b],
                                                  dsts=[b] * len(ids), alu_op=0)], local_sem=T.sem["lv_%d" % t])
        g.wait_ge(T.sem.la0, len(topo.engines(core, peers[0])))
        for t in range(STEPS):
            g.wait_ge(T.sem["lv_%d" % t], len(topo.engines(core, far[0])))


def rank_program(g, core, T, topo):
    rank = T.rank_of(core)
    if rank is None:
        helper_program(g, core, T, topo)
        return
    Q = {"v": g.vector, "s": g.scalar, "p": g.tensor, "g": g, "y": g.sync}
    SEM = {"v": "sv", "s": "ss", "p": "sp", "g": "sg"}
    ops = []
    hist = {}
    ndma = [0]

    def B(name, c0=0, c1=None, step=1, p0=0, p1=128):
        if c1 is None:
            c1 = SCRATCH[name][1][1]
        return (name, p0, p1, c0, c1, step)

    def ap(b):
        if b[5] == 1:
            return T[b[0]][b[1]:b[2], b[3]:b[4]]
        return T[b[0]][b[1]:b[2], b[3]:b[4]:b[5]]

    def record(q, kind, fn, outs, ins, cost, lat, tok=None, pre=(), after=()):
        me = len(ops)
        preds = {}
        for b, w in [(o, True) for o in outs] + [(i, False) for i in ins]:
            bank = b[0] in PSUM
            for (c0, c1, hw, i, st) in hist.get(b[0], []):
                hq, hk = ops[i]["q"], ops[i]["kind"]
                apart = c1 <= b[3] or b[4] <= c0 or (st == b[5] and (c0 - b[3]) % st != 0)
                same = hq == q and hk == "c" and kind == "c"
                if bank and q == "p" and hq == "p":
                    preds.setdefault(i, False)
                    continue
                if apart and not (bank and not same):
                    continue
                if not (w or hw) and not (bank and not same):
                    continue
                preds[i] = True
        ops.append({"q": q, "kind": kind, "fn": fn, "preds": preds, "cost": cost, "lat": lat, "tok": tok, "pre": list(pre), "after": list(after)})
        for b, w in [(o, True) for o in outs] + [(i, False) for i in ins]:
            keep = []
            for e in hist.get(b[0], []):
                if w and b[5] == 1 and b[2] - b[1] == 128 and b[3] <= e[0] and e[1] <= b[4] and b[0] not in PSUM:
                    continue
                if b[0] in PSUM and e[2] == w and ops[e[3]]["q"] == q and e[0] == b[3] and e[1] == b[4] and e[4] == b[5] and (w and q == "p"):
                    continue
                keep.append(e)
            keep.append((b[3], b[4], w, me, b[5]))
            hist[b[0]] = keep
        return me

    def op(q, fn, outs, ins, cost, pre=(), after=()):
        return record(q, "c", fn, outs, ins, cost, WAKE, None, pre, after)

    def dma(q, out, in_, outs, ins, nbytes):
        sem = "d%d" % ndma[0]
        ndma[0] += 1
        return record(q, "d", lambda: Q[q].dma_start(out, in_), outs, ins, 0.1, 2.0 + nbytes / 2e5, (sem, 16))

    def emit():
        n = len(ops)
        succ = [[] for _ in range(n)]
        left = [0] * n
        for j in range(n):
            es = [(i, ops[i]["lat"] if w else 0.0) for i, w in ops[j]["preds"].items()] + ops[j]["after"]
            left[j] = len(es)
            for i, l in es:
                succ[i].append((j, l))
        prio = [0.0] * n
        for i in range(n - 1, -1, -1):
            prio[i] = ops[i]["cost"] + max([prio[j] + l for j, l in succ[i]] + [ops[i]["lat"] if ops[i]["kind"] == "d" else 0.0])
        rdy = [0.0] * n
        cand = {q: [i for i in range(n) if not left[i] and ops[i]["q"] == q] for q in Q}
        free = {q: 0.0 for q in Q}
        order = []
        while len(order) < n:
            best = None
            for q in Q:
                if not cand[q]:
                    continue
                e0 = max(free[q], min(rdy[i] for i in cand[q]))
                i = max([i for i in cand[q] if rdy[i] <= e0 + 1e-9], key=lambda i: (prio[i], -i))
                if best is None or e0 < best[0]:
                    best = (e0, q, i)
            e0, q, i = best
            cand[q].remove(i)
            order.append(i)
            free[q] = e0 + ops[i]["cost"]
            for j, l in succ[i]:
                rdy[j] = max(rdy[j], free[q] + l)
                left[j] -= 1
                if not left[j]:
                    cand[ops[j]["q"]].append(j)
        clock = {q: {} for q in Q}
        snap, held = {}, {}
        cnt = {q: 0 for q in Q}

        def wait(q, sem, val):
            if clock[q].get(sem, 0) >= val:
                return
            Q[q].wait_ge(T.sem[sem], val)
            for k, v in snap.get((sem, val), {}).items():
                if clock[q].get(k, 0) < v:
                    clock[q][k] = v
            clock[q][sem] = val

        for i in order:
            o = ops[i]
            q = o["q"]
            need = {}
            for sem, val in o["pre"] + [ops[j]["tok"] for j, w in o["preds"].items() if w]:
                need[sem] = max(need.get(sem, 0), val)
            for sem in sorted(need):
                wait(q, sem, need[sem])
            r = o["fn"]()
            if o["kind"] == "c":
                cnt[q] += 1
                o["tok"] = (SEM[q], cnt[q])
                r.then_inc(T.sem[SEM[q]], 1)
            elif o["kind"] == "d":
                r.then_inc(T.sem[o["tok"][0]], 16)
            snap[o["tok"]] = dict(clock[q])
            held[o["tok"][0]] = max(held.get(o["tok"][0], 0), o["tok"][1])
        for sem in sorted(held):
            wait("g", sem, held[sem])

    CYC = 0.001

    def wd(b):
        return (b[4] - b[3] + b[5] - 1) // b[5]

    def two(*bs):
        return all(SCRATCH[b[0]][2] in ("bfloat16", "uint16") for b in bs if wd(b) > 1)

    def cp(o, i):
        op("v", lambda: g.vector.tensor_copy(ap(o), ap(i)), [o], [i], CYC * max(64, wd(o) * (0.5 if two(o, i) else 1)))

    def tt(o, a, b, f):
        op("v", lambda: g.vector.tensor_tensor(ap(o), ap(a), ap(b), f), [o], [a, b],
           CYC * max(64, wd(o) * (1 if a[0] in PSUM or b[0] in PSUM else 2)))

    def ts(o, a, s1, f1, s2=None, f2=None):
        x1 = ap(s1) if isinstance(s1, tuple) else s1
        x2 = ap(s2) if isinstance(s2, tuple) else s2
        ins = [a] + [s for s in (s1, s2) if isinstance(s, tuple)]
        c = CYC * max(64, wd(o) * (0.5 if two(o, a) else 1))
        if f2 is None:
            op("v", lambda: g.vector.tensor_scalar(ap(o), ap(a), x1, None, f1), [o], ins, c)
        else:
            op("v", lambda: g.vector.tensor_scalar(ap(o), ap(a), x1, x2, f1, f2), [o], ins, c)

    def fill(o, c):
        op("v", lambda: g.vector.memset(ap(o), c), [o], [], CYC * max(64, wd(o) * (0.5 if two(o) else 1)))

    def scan(o, d0, d1, f0, f1):
        op("v", lambda: g.vector.tensor_tensor_scan(ap(o), ap(d0), ap(d1), 0.0, f0, f1), [o], [d0, d1],
           CYC * max(64, wd(o) * (0.5 if two(o, d0, d1) else 1)))

    def act(o, i, f, bias=0.0, scale=1.0):
        op("s", lambda: g.scalar.activation(ap(o), ap(i), f, bias=bias, scale=scale), [o], [i], CYC * max(64, wd(o)))

    def mm(o, l, r, st, sp):
        op("p", lambda: g.tensor.matmul(ap(o), ap(l), ap(r), st, sp), [o], [l, r],
           0.00085 * max(min(64, wd(l)), wd(r)) * (4 if SCRATCH[l[0]][2] == "float32" else 1))

    def iota(o, pat, base, cm):
        op("g", lambda: g.iota(ap(o), pat, base, cm), [o], [], 0.2 + 2 * CYC * wd(o))

    def gather(q, o, w, off, pre=(), after=()):
        c = 0.06 + 1.5 * CYC * wd(o)
        if q == "v":
                op("v", lambda: g.vector.tensor_copy(ap(o), ap(w).indirect(ap(off))), [o], [w, off], c, pre, after)
        else:
            op("s", lambda: g.scalar.activation(ap(o), ap(w).indirect(ap(off)), AF.Copy), [o], [w, off], c, pre, after)

    def scatter(q, w, off, i, pre=(), after=()):
        c = 0.06 + 3.8 * CYC * wd(i)
        if q == "v":
            op("v", lambda: g.vector.tensor_copy(ap(w).indirect(ap(off)), ap(i)), [w], [off, i], c, pre, after)
        else:
            op("s", lambda: g.scalar.activation(ap(w).indirect(ap(off)), ap(i), AF.Silu), [w], [off, i], c, pre, after)

    def sm(k):
        return B("sm", 16 * k, 16 * k + 16)

    def si(k):
        return B("si", 16 * k, 16 * k + 16)

    def ends(n):
        return B(n, 15, 256, 16)

    def starts(n):
        return B(n, 0, 256, 16)

    win, winb, wval = B("win"), B("winb"), B("win", VAL, WC)
    own, own_up = [B(n, rank * C, rank * C + C) for n in ("winb", "win")]

    def send(b, sem, loc):
        others = [c for c in T.cores if c != core]
        nb = wd(b) * 256
        far = [c for c in others if topo.chip(c) != topo.chip(core)]
        near = [c for c in others if topo.chip(c) == topo.chip(core)]
        ef = topo.engines(core, far[0])
        en = [e for e in topo.engines(core, near[0]) if e not in ef]
        trs = []
        for dst, eng in ((far, ef), (near, en)):
            ids = []
            for c in dst:
                rid, pid, _ = topo.addr(c)
                ids.append(DstId(rid=rid, pnc=pid))
            trs.append(RemoteDMATransfer(dst_ids=ids, dma_engine_mask=sum(1 << e for e in eng), remote_sem=T.sem[sem],
                                         srcs=[ap(b)], dsts=[ap(b)] * len(ids), alu_op=0))
        lat = 2.5 + nb / 2e4
        return record("g", "r", lambda: g.remote_dma_fused(trs, local_sem=T.sem[loc]), [], [b], 1.0, lat, (loc, len(ef) + len(en))), lat

    def arrives(src):
        if src == core:
            return 0
        ef = topo.engines(src, [c for c in T.cores if topo.chip(c) != topo.chip(src)][0])
        if topo.chip(src) != topo.chip(core):
            return len(ef)
        return len([e for e in topo.engines(src, core) if e not in ef])

    dma("y", ap(own), T.mem[:], [own], [], 262144)
    dma("s", T.hb0[:], T.h[:], [B("hb0")], [], 65536)
    dma("y", T.praw[:], T.pnd[:], [B("praw")], [], 131072)
    dma("s", T.draw[:], T.due[:], [B("draw")], [], 131072)
    dma("y", T.wraw[:, 0:1], T.w[:], [B("wraw")], [], 512)
    dma("s", T.kraw[:, 0:1], T.kap[:], [B("kraw")], [], 512)
    dma("y", T.traw[:, 0:1], T.th[:], [B("traw")], [], 512)
    dma("s", T.vali[:], T.val[:], [B("vali")], [], 1048576)
    iota(B("iotp", 0, 1), [[0, 1]], 0, 1)
    iota(B("iotc"), [[1, 256]], 0, 0)
    mates_, rows = chip_ranks(T, topo, core), [B("winb", r * C, r * C + C) for r in range(N)]
    sib = [c for c in mates_ if c != core][0]
    peers = far_peers(T, topo, core)
    helper = helper_of(T, topo, core)
    ef = topo.engines(core, peers[0])
    en = [e for e in topo.engines(core, sib) if e not in ef]
    lo, hi = B("winb", rank * C, rank * C + SPLIT), B("winb", rank * C + SPLIT, rank * C + C)

    def transfer(dsts, eng, sem, b):
        ids = []
        for c in dsts:
            rid, pid, _ = topo.addr(c)
            ids.append(DstId(rid=rid, pnc=pid))
        return RemoteDMATransfer(dst_ids=ids, dma_engine_mask=sum(1 << e for e in eng), remote_sem=T.sem[sem],
                                 srcs=[ap(b)], dsts=[ap(b)] * len(ids), alu_op=0), len(eng)

    def fused(trs, bs, loc, lat, pre=(), after=()):
        count = sum(n for _, n in trs)
        return record("g", "r", lambda: g.remote_dma_fused([x for x, _ in trs], local_sem=T.sem[loc]), [], bs, 1.0, lat, (loc, count), pre, after)

    first = fused([transfer([helper], en, "hp", hi)], [hi], "la0", 3.0)
    second = fused([transfer(peers, ef, "ag1", lo), transfer([sib], en, "agr", lo)], [lo], "la1", 8.0)
    fused([transfer([sib], en, "agr", hi)], [hi], "la2", 3.0)
    srcs = [T.rank_of(c) for c in peers]
    ch = topo.engines(core, sib)
    k4 = len(ch) // 4
    got = [("ag1", len(ef) * len(peers)), ("ag2", len(ef) * len(peers))]
    relays = []
    for z in range(2):
        bs = [B("winb", r * C + (0, SPLIT)[z], r * C + (SPLIT, C)[z]) for r in srcs]
        trs = [transfer([sib], ch[k4 * x:k4 * x + k4], "agr", b) for x, b in enumerate(bs)]
        relays.append((fused(trs, bs, "lr%d" % z, 3.5, [got[z]], [((second, 8.0), (first, 9.5))[z]]), 3.5))
    got.append(("agr", 2 * len(en) + 2 * len(peers) * k4))

    PF, PG, PM, PS, WCOL, KCOL, TCOL = [B("colf", k, k + 1) for k in range(7)]
    cp(PF, B("iotp", 0, 1))
    ts(B("coli", 0, 1), B("iotp", 0, 1), 4, A.arith_shift_right)
    ts(B("coli", 1, 2), B("iotp", 0, 1), 15, A.bitwise_and)
    ts(B("cg"), B("iotc"), 4, A.arith_shift_right)
    ts(B("cm"), B("iotc"), 15, A.bitwise_and)
    cp(PG, B("coli", 0, 1))
    cp(PM, B("coli", 1, 2))
    ts(PS, PM, 1.0 / 512, A.mult)
    ts(B("idf"), B("iotc", 0, 128), PF, A.is_equal)
    ts(B("idb"), B("iotc", 0, 128), PF, A.is_equal)
    ts(B("bob"), B("cg", 0, 128), PG, A.is_equal)
    ts(B("gib"), B("iotc", 0, 8), PG, A.is_equal)
    ts(B("gif"), B("iotc", 0, 8), PG, A.is_equal)
    ts(B("r01"), B("cm"), 0, A.not_equal)
    ts(B("dm"), B("cm"), PM, A.is_equal)
    cp(B("tmp1"), B("praw"))
    ts(B("tmp2"), B("draw"), 1.0 / 32, A.mult, PS, A.add)
    for q in range(2):
        mm(B("ps", 128 * q, 128 * q + 128), B("tmp1", 128 * q, 128 * q + 128), B("idf"), True, True)
        mm(B("ps", 256 + 128 * q, 384 + 128 * q), B("tmp2", 128 * q, 128 * q + 128), B("idf"), True, True)
    act(B("nmd"), B("ps", 0, 256), AF.Copy)
    act(B("dk"), B("ps", 256, 512), AF.Copy)
    ts(B("onesb"), B("idb"), 0.0, A.mult, 1.0, A.add)
    fill(B("onesf"), 1.0)
    cp(WCOL, B("wraw", 0, 1))
    cp(KCOL, B("kraw", 0, 1))
    cp(TCOL, B("traw", 0, 1))
    fill(B("we"), 0.0)
    for q in range(2):
        for z in (0, 32):
            ts(B("we", 48 * q + z + 8 * q, 48 * q + z + 8 * q + 8), B("gib"), WCOL, A.mult)
    ts(B("zi"), B("cm"), 1, A.bitwise_and)
    cp(B("oc"), B("zi"))
    ts(B("tmp3", 0, 128), B("idf"), KCOL, A.mult)
    ts(B("tmp3", 128, 136), B("gif"), TCOL, A.mult, 1.0 / 16, A.mult)
    mm(B("pk", 0, 128), B("onesf"), B("tmp3", 0, 128), True, True)
    mm(B("pk", 128, 136), B("onesf"), B("tmp3", 128, 136), True, True)
    for q in range(2):
        o = B("mz", 128 * q, 128 * q + 128, 1, 0, 48)
        x = B("off", 128 * q, 128 * q + 128, 1, 0, 48)
        cgs = B("cg", 0, 128, 1, 0, 48)
        pfs = B("colf", 0, 1, 1, 0, 48)
        ts(o, cgs, 8.0 * q, A.add, pfs, A.is_equal)
        tt(o, B("pk", 0, 128, 1, 0, 48), o, A.mult)
        ts(x, cgs, 8.0 * q + 32, A.add, pfs, A.is_equal)
        tt(o, o, x, A.add)
        zo, ze = [B(n, 128 * q, 128 * q + 128, 1, 0, 48) for n in ("lzo", "lze")]
        tt(zo, o, B("oc", 0, 128, 1, 0, 48), A.mult)
        tt(ze, o, zo, A.subtract)
        cp(B("thd", 8 * q, 8 * q + 8), B("pk", 128, 136))
    fill(B("rz"), 0.0)
    fill(B("acol"), 0.0)
    cp(B("zi"), B("nmd"))
    ts(B("a0"), B("zi"), 7, A.arith_shift_right)
    ts(B("bit"), B("zi"), 127, A.bitwise_and)
    cp(B("hid"), B("a0"))
    cp(B("r1", 1, 256, 2), B("bit", 0, 256, 2))
    cp(B("r2", 1, 256, 2), B("bit", 1, 256, 2))
    tt(B("nmo"), B("nmd"), B("oc"), A.mult)
    ts(B("w8", 0, 8), B("iotc", 0, 16, 2), PM, A.is_equal, 128.0, A.mult)
    ts(B("w8", 8, 16), B("iotc", 1, 16, 2), PM, A.is_equal)
    tt(B("w8", 16, 24), B("w8", 0, 8), B("w8", 8, 16), A.add)
    for q in range(8):
        ts(B("bs", 128 * q, 128 * q + 128), B("bob"), B("w8", 16 + q, 17 + q), A.mult)
    for s in range(S):
        ts(B("wh", 128 * s, 128 * s + 128), B("idb"), 256.0 * (64 + s), A.mult)
    fill(B("cy", 0, 256, 1, 0, 2), VAL - 16384.0)
    cp(B("cy", 0, 256, 1, 0, 1), B("iotc", 0, 256, 1, 0, 1))
    ts(B("ckf", 0, 128, 1, 0, 1), B("cm", 0, 128, 1, 0, 1), -1.0 / 16, A.mult, 15.0 / 16, A.add)
    ts(B("ck16", 0, 128, 1, 0, 1), B("cm", 0, 128, 1, 0, 1), 16384.0, A.mult)
    ts(B("tri"), B("cm"), PM, A.is_gt)
    ts(B("nidb"), B("idb"), -1.0, A.mult)
    ts(B("n2idb"), B("idb"), -2.0, A.mult)
    ts(B("ngib"), B("gib"), -1.0, A.mult)
    ts(sm(0), B("iotc", 0, 16), 16.0, A.mult, PM, A.add)
    ts(sm(1), sm(0), 1.0 * PL, A.add)
    for t in range(STEPS):
        ts(sm(2 + t), sm(0), 1.0 * VAL + TH * t, A.add)
    fill(B("rstp"), 0.0)
    fill(B("rstn"), 0.0)
    fill(B("rstp", 0, 1024, 16), 256.0)
    fill(B("rstn", 0, 1024, 16), -256.0)
    for k in range(5):
        fill(B("zz%d" % k), 0.0)
    fill(B("zc"), 0.0)

    def spread_h(h):
        for k in range(S):
            act(B("hexp", k, 4096, 16), h, AF.Copy)

    spread_h(B("hb0"))
    for s in range(S):
        act(B("winb", VAL + TH * s, VAL + TH * s + TH), B("vali", s, 4096, 16), AF.Copy)
    for s in range(S):
        act(B("win", VAL + TH * s, VAL + TH * s + TH), B("vali", s, 4096, 16), AF.Identity, UP)

    def bcast(dst, k):
        scan(dst, B("r01"), B("zz%d" % k), A.mult, A.add)

    def to_lists(dst, src_m):
        for q in range(2):
            mm(B(dst[0], dst[3] + 8 * q, dst[3] + 8 * q + 8), B(src_m, 128 * q, 128 * q + 128), B("gif"), True, True)

    def scatter_all(t, sent):
        for r in range(N - 1, -1, -1):
            lv, ln = B("lv%d" % t, TH * r, TH * r + TH), B("ln%d" % t, 16 * r, 16 * r + 16)
            nv = 2 * len(ef) if topo.chip(T.cores[r]) != topo.chip(core) else len(en) // 2 + len(en) // 4
            cv, cn = [[] if r == rank else [(n + "%d_%d" % (t, r), k)] for n, k in (("x", nv), ("n", arrives(T.cores[r])))]
            if t + 1 == STEPS:
                scatter("v", B("winb", 0, VAL), ln, lv, cv + cn, sent)
            else:
                lf = B("lvf", TH * r, TH * r + TH)
                op("v", lambda o=lf, i=lv: g.vector.tensor_copy(ap(o), ap(i)), [lf], [lv], CYC * TH, cv, sent[:1])
                scatter("s", B("win", 0, VAL), ln, lf, cn, sent[1:])

    def early_drain(t):
        scan(B("km"), B("rstp", 0, 256), B("dk"), A.add, A.min)
        cp(starts("zz0"), ends("km"))
        bcast(B("pv", 0, 256), 0)
        tt(B("oh"), B("pv", 0, 256), B("dk"), A.is_equal)
        tt(B("pv", 256, 512), B("oh"), B("nmd"), A.mult)
        scan(B("wb"), B("r01"), B("pv", 256, 512), A.mult, A.add)
        ts(starts("zz1"), ends("wb"), 1.0, A.add)
        bcast(B("tmp1"), 1)
        for q in range(2):
            mm(B("pz", 128 * q, 128 * q + 128), B("tmp1", 128 * q, 128 * q + 128), B("idf"), True, True)
        ts(si(0), ends("km"), 512.0, A.mult)
        ts(si(1), si(0), 15, A.bitwise_and)
        ts(sm(6), ends("km"), (t + 1) / 32.0, A.is_lt)
        ts(sm(7), ends("km"), 31.0 / 32, A.is_lt)
        ts(sm(8), si(1), 8192.0, A.mult)
        ts(sm(9), sm(6), 131072.0, A.mult)
        ts(sm(10), sm(7), 262144.0, A.mult)
        tt(sm(8), sm(8), ends("wb"), A.add)
        tt(sm(9), sm(9), sm(10), A.add)
        tt(starts("zz2"), sm(8), sm(9), A.add)
        bcast(B("pv", 0, 256), 2)
        tt(B("wm"), B("pv", 0, 256), B("dm"), A.mult)
        to_lists(B("pz", 256, 272), "wm")
        cp(B("pbu"), B("pz", 0, 256))
        tt(B("pbm"), B("pz", 0, 256), B("tri"), A.mult)
        cp(si(2), B("pz", 256, 272))
        ts(si(3), si(2), 8191, A.bitwise_and)
        ts(si(4), si(2), 13, A.arith_shift_right, 15, A.bitwise_and)
        ts(si(5), si(2), 17, A.arith_shift_right, 1, A.bitwise_and)
        ts(si(6), si(2), 18, A.arith_shift_right, 1, A.bitwise_and)
        ts(sm(11), si(4), 256.0, A.mult)
        tt(sm(11), sm(11), sm(0), A.add)
        cp(B("l2"), sm(11))
        ts(sm(12), si(3), 2.0, A.add)
        tt(sm(13), si(3), sm(1), A.subtract)

    for t in range(STEPS):
        h, hn = B("hb%d" % (t % 2)), B("hb%d" % ((t + 1) % 2))
        ts(B("pv", 0, 256), B("dk"), 31.0 / 32, A.is_ge, -128.0, A.mult)
        tt(B("r1", 0, 256, 2), B("pv", 0, 256, 2), B("hid", 0, 256, 2), A.add)
        tt(B("r2", 0, 256, 2), B("pv", 1, 256, 2), B("hid", 1, 256, 2), A.add)
        for q in range(2):
            mm(B("pk", 0, 128, 1, 0, 48), B("we", 48 * q, 48 * q + 48), B(h[0], 128 * q, 128 * q + 128), q == 0, q == 1)
        for q in range(2):
            mm(B("ps", 128 * q, 128 * q + 128), B("r1", 128 * q, 128 * q + 128), B("idb"), True, True)
        for q in range(2):
            mm(B("ps", 256 + 128 * q, 384 + 128 * q), B("r2", 128 * q, 128 * q + 128), B("idb"), True, True)
        act(B("r1a"), B("ps", 0, 256), AF.Copy)
        act(B("r2a"), B("ps", 256, 512), AF.Copy)
        u48 = B("ui", 0, 128, 1, 0, 48)
        cp(u48, B("pk", 0, 128, 1, 0, 48))
        m48 = B("um", 0, 128, 1, 0, 48)
        ts(m48, u48, 4095, A.bitwise_and)
        hi16 = B("um", 0, 128, 1, 32, 48)
        q16 = B("usq", 0, 128, 1, 32, 48)
        s16 = B("ui", 0, 128, 1, 32, 48)
        tt(q16, hi16, hi16, A.mult)
        cp(B("rz", 0, 128, 1, 0, 16), B("um", 0, 128, 1, 0, 16))
        ts(s16, q16, 4, A.arith_shift_right)
        ts(B("rz", 0, 128, 1, 32, 48), s16, B("acol", 0, 1, 1, 32, 48), A.add)
        rz = B("rz", 0, 128, 1, 0, 48)
        for q in range(2):
            mm(B("pz", 128 * q, 128 * q + 128), B("lzo", 128 * q, 128 * q + 128, 1, 0, 48), rz, True, True)
        for q in range(2):
            o = B("pz", 256 + 128 * q, 384 + 128 * q)
            mm(o, B("nmo", 128 * q, 128 * q + 128), B("idf"), True, False)
            mm(o, B("lze", 128 * q, 128 * q + 128, 1, 0, 48), rz, False, True)

        def names(j):
            for z in range(2):
                s = 2 * j + z
                mm(B(("pa", "pb", "pc")[j % 3], 256 * z, 256 * z + 256), B("bs", 128 * j, 128 * j + 128), B(("r1a", "r2a")[z]), True, True)
        for j in range(3):
            names(j)
        cp(B("zi"), B("pz", 0, 256))
        ts(B("bit"), B("zi"), 3, A.arith_shift_right, 1, A.bitwise_and)
        tt(B("mz"), B("bit"), B("pz", 0, 256), A.mult)
        tt(B("a0"), B("mz"), B("pz", 256, 512), A.add)
        ts(B("ai"), B("a0"), 8191, A.bitwise_and)
        mm(B("py", 0, 256), B("onesb", 0, 128, 1, 0, 2), B("cy", 0, 256, 1, 0, 2), True, False)
        for j in range(8):
            for z in range(2):
                s = 2 * j + z
                tt(B("eqb", 256 * s, 256 * s + 256), B(("pa", "pb", "pc")[j % 3], 256 * z, 256 * z + 256), B("ai"), A.is_equal)
            if j + 3 < 8:
                names(j + 3)
            for z in range(2):
                s = 2 * j + z
                mm(B("py", 0, 256), B("wh", 128 * s, 128 * s + 128), B("eqb", 256 * s, 256 * s + 256), False, s == S - 1)
        tt(B("off"), B("py", 0, 256), B("ai"), A.max)
        cp(B("ou", 128, 256), B("off", 128, 256))
        cp(B("ou", 0, 128), B("off", 0, 128))
        for q in range(2):
            o = B("py", 256 + 128 * q, 384 + 128 * q)
            mm(o, B("onesb", 0, 128, 1, 0, 1), B("ck16", 0, 128, 1, 0, 1), True, False)
            mm(o, B("off", 128 * q, 128 * q + 128), B("idf"), False, True)
        early_drain(t)
        pre, after, up = [], [], UP
        src = win
        if t == 0:
            pre, after, up, src = got, relays, 0.0, winb
        for q, c0, c1 in PARTS:
            gather(q, B("xs", 16 * c0, 16 * c1), src, B("ou", c0, c1), pre, after)
        if t == 0:
            for r in range(N):
                o, i = B("win", C * r, C * r + C), B("winb", C * r, C * r + C)
                op("s", lambda o=o, i=i: g.scalar.activation(ap(o), ap(i), AF.Identity, bias=UP, scale=1.0), [o], [i], CYC * C, pre, after)
        for b in ORDER:
            c0 = 512 * b
            bank = B(("pa", "pb", "pc")[ORDER.index(b) % 3])
            mm(bank, B("idb"), B("xs", c0, c0 + 512), True, False)
            mm(bank, B("nidb"), B("hexp", c0, c0 + 512), False, True)
            act(B("ab", c0, c0 + 512), bank, AF.Abs, -up)
        for q in range(2):
            mm(B("pk", 128 * q, 128 * q + 128), B("onesb", 0, 128, 1, 0, 1), B("ckf", 0, 128, 1, 0, 1), True, False)
            for k in range(S):
                mm(B("pk", 128 * q + k, 128 * q + 128, 16), B("ab", 2048 * q + k, 2048 * q + 2048, 16), B("gib"), False, k == S - 1)
        for q in range(4):
            scan(B("hs", 1024 * q, 1024 * q + 1024), B("rstn"), B("xs", 1024 * q, 1024 * q + 1024), A.add, A.max)
            scan(B("lsc", 1024 * q, 1024 * q + 1024), B("rstp"), B("xs", 1024 * q, 1024 * q + 1024), A.add, A.min)
        for q in range(2):
            hq, lq = B("hs", 2048 * q + 15, 2048 * q + 2048, 16), B("lsc", 2048 * q + 15, 2048 * q + 2048, 16)
            mm(B("ps", 8 * q, 8 * q + 8), hq, B("gib"), True, False)
            mm(B("ps", 8 * q, 8 * q + 8), lq, B("ngib"), False, True)
            s2 = B("pb", 128 * q, 128 * q + 128)
            mm(s2, B("idb"), hq, True, False)
            mm(s2, B("idb"), lq, False, False)
            mm(s2, B("n2idb"), B(h[0], 128 * q, 128 * q + 128), False, True)
        act(B("yd"), B("pb", 0, 256), AF.Identity, 191.875 - up, 0.5)
        for q in range(2):
            o = B("pc", 128 * q, 128 * q + 128)
            mm(o, B("idb"), B("yd", 128 * q, 128 * q + 128), True, False)
            mm(o, B("idb"), B(h[0], 128 * q, 128 * q + 128), False, True)
            o = B("ps", 16 + 8 * q, 24 + 8 * q)
            mm(o, B("yd", 128 * q, 128 * q + 128), B("gib"), True, False)
            mm(o, B(h[0], 128 * q, 128 * q + 128), B("gib"), False, True)
        act(B("yb"), B("pc", 0, 256), AF.Identity, UP - 192.0)
        act(hn, B("yd"), AF.Abs, -192.0)
        scan(B("km2"), B("r01"), B("pk", 0, 256), A.mult, A.max)
        tt(B("rec"), B("pk", 0, 256), B("km2"), A.is_equal)
        tt(B("ro"), B("py", 256, 512), B("rec"), A.mult)
        scan(B("os"), B("r01"), B("ro"), A.mult, A.max)
        tt(sm(14), B("ps", 0, 16), B("thd"), A.is_ge)
        cp(si(7), ends("os"))
        ts(sm(15), sm(14), 1.0 * DUM, A.mult)
        ts(si(8), si(7), 16383, A.bitwise_and)
        best = starts("zz3")
        tt(best, si(8), sm(15), A.max)
        bcast(B("pv", 0, 256), 3)
        tt(B("wm2"), B("pv", 0, 256), B("dm"), A.mult)
        to_lists(B("ps", 32, 48), "wm2")
        w = sm(17)
        cp(w, B("ps", 32, 48))
        tt(sm(18), w, sm(2 + t), A.subtract)
        ts(sm(19), w, 1.0 * VAL, A.is_ge)
        ts(sm(20), w, 1.0 * DUM, A.is_ge)
        tt(sm(21), sm(18), sm(19), A.mult)
        tt(sm(22), sm(20), sm(0), A.mult)
        tt(sm(23), sm(21), sm(2 + t), A.add)
        tt(sm(24), sm(23), sm(22), A.add)
        ts(B("stl"), sm(24), -1.0 * VAL, A.add)
        scatter("v", wval, B("stl"), B("yb"))
        lv, ln = B("lv%d" % t, TH * rank, TH * rank + TH), B("ln%d" % t, 16 * rank, 16 * rank + 16)
        gather("v", lv, wval, B("l2"))
        l0, l1 = B(lv[0], lv[3], lv[3] + 128), B(lv[0], lv[3] + 128, lv[4])
        far = [c for c in T.cores if topo.chip(c) != topo.chip(core)]
        xs = "x%d_%d" % (t, rank)
        k2 = len(en) // 2
        vt = [transfer(far, ef, xs, l0), transfer([sib], en[:k2], xs, l0), transfer([sib], en[k2:k2 + k2 // 2], xs, l1),
              transfer([helper], en[k2 + k2 // 2:], "hv%d" % t, l1)]
        sent = [(fused(vt, [l0, l1], "lv_%d" % t, 6.0), 6.0)]
        tt(sm(25), si(6), sm(20), A.mult)
        tt(sm(26), si(5), sm(25), A.max)
        tt(sm(27), sm(12), sm(26), A.mult)
        ts(starts("zc"), sm(27), -1.0, A.add)
        scan(B("pv", 0, 256), B("r01"), B("zc"), A.mult, A.add)
        eb = B("eb", 0, 256)
        tt(eb, B("pv", 0, 256), B("pbm"), A.is_equal)
        mm(B("pz", 0, 256), B("bob"), eb, True, False)
        e0 = 256
        for c in range(15):
            n = 256 - 16 * (c + 1)
            eb = B("eb", e0, e0 + n)
            e0 += n
            ts(eb, B("pbu", 256 - n, 256), B("zc", 16 * c, 16 * c + 1), A.is_equal)
            mm(B("pz", 256 - n, 256), B("bob"), eb, False, c == 14)
        tt(B("pv", 256, 512), B("pz", 0, 256), B("dm"), A.mult)
        scan(B("dsc"), B("r01"), B("pv", 256, 512), A.mult, A.add)
        ts(sm(29), ends("dsc"), 0.5, A.is_lt)
        tt(sm(30), sm(29), sm(26), A.mult)
        tt(sm(31), sm(30), sm(13), A.mult)
        tt(sm(32), sm(31), sm(1), A.add)
        cp(ln, sm(32))
        sent.append(send(ln, "n%d_%d" % (t, rank), "ln_%d" % t))
        if t + 1 < STEPS:
            spread_h(hn)
            scatter_all(t, sent)
        tt(sm(33), sm(7), sm(14), A.mult)
        tt(starts("zz4"), sm(6), sm(33), A.max)
        bcast(B("pv", 0, 256), 4)
        tt(B("pv", 256, 512), B("pv", 0, 256), B("oh"), A.mult)
        tt(B("dk"), B("dk"), B("pv", 256, 512), A.add)
        ts(sm(34), best, 1.0 * VAL, A.is_lt)
        cp(si(9), B("ps", 16, 32))
        ts(si(10), si(9), 1, A.bitwise_and)
        ts(sm(35), si(10), 1.0 / 32, A.mult, (t - 30) / 32.0, A.add)
        tt(sm(35), sm(35), sm(34), A.mult)
        dt_, nt_ = B("dk", t, 256, 16), B("nmd", t, 256, 16)
        tt(dt_, dt_, sm(35), A.add)
        tt(sm(36), best, nt_, A.subtract)
        tt(sm(36), sm(36), sm(34), A.mult)
        tt(nt_, nt_, sm(36), A.add)
        if t + 1 < STEPS:
            cp(si(11), nt_)
            ts(si(12), si(11), 7, A.arith_shift_right)
            ts(si(13), si(11), 127, A.bitwise_and)
            cp(B("hid", t, 256, 16), si(12))
            if t % 2 == 0:
                cp(B("r1", t + 1, 256, 16), si(13))
            else:
                cp(B("r2", t, 256, 16), si(13))
                cp(B("nmo", t, 256, 16), nt_)
            ac = B("acol", 1, 2)
            op("v", lambda ac=ac: g.vector.tensor_reduce(ap(ac), ap(sm(14)), AxisListType.X, A.add), [ac], [sm(14)], CYC * 64)
            mm(B("ps", 48, 49), B("onesf"), ac, True, True)
            cp(B("coli", 2, 3), B("ps", 48, 49))
            ts(B("coli", 3, 4), B("coli", 2, 3), 63, A.bitwise_and)
            cp(B("acol", 0, 1), B("coli", 3, 4))
    hl = "hb%d" % (STEPS % 2)
    act(B("winb", rank * C, rank * C + C), own_up, AF.Copy)
    dma("y", T.yh[:], T[hl][:], [], [B(hl)], 65536)
    ts(B("zi"), B("dk"), 512.0, A.mult)
    ts(B("bit"), B("zi"), 4, A.arith_shift_right)
    ts(B("tmp1"), B("bit"), 31.0, A.min)
    for q in range(2):
        mm(B("ps", 128 * q, 128 * q + 128), B("nmd", 128 * q, 128 * q + 128), B("idf"), True, True)
        mm(B("ps", 256 + 128 * q, 384 + 128 * q), B("tmp1", 128 * q, 128 * q + 128), B("idf"), True, True)
    act(B("onm"), B("ps", 0, 256), AF.Copy)
    act(B("odu"), B("ps", 256, 512), AF.Copy)
    dma("y", T.ypnd[:], T.onm[:], [], [B("onm")], 131072)
    dma("y", T.ydue[:], T.odu[:], [], [B("odu")], 131072)
    for s in range(S):
        act(B("vali", s, 4096, 16), B("win", VAL + TH * s, VAL + TH * s + TH), AF.Identity, -UP)
    dma("s", T.yval[:], T.vali[:], [], [B("vali")], 1048576)
    scatter_all(STEPS - 1, sent)
    ts(B("ab", 0, C), own, -UP, A.add)
    dma("y", T.ymem[:], T.ab[:, 0:C], [], [B("ab", 0, C)], 262144)
    emit()
